import numpy as np
import ml_dtypes


def mxq(x, axis, fmt="e4m3"):
    dtype, down = {"e4m3": (ml_dtypes.float8_e4m3fn, 7), "e5m2": (ml_dtypes.float8_e5m2, 14)}[fmt]
    v = np.moveaxis(np.asarray(x, np.float32).astype(ml_dtypes.bfloat16).astype(np.float64), axis, -1)
    blocks = v.reshape(v.shape[:-1] + (-1, 32))
    amax = np.abs(blocks).max(-1, keepdims=True)
    byte = np.maximum(np.where(amax > 0, np.frexp(amax)[1] - 1 + 127, 0) - down, 1)
    scale = np.exp2(byte - 127.0)
    codes = (blocks / scale).astype(np.float32).astype(dtype).astype(np.float64)
    return np.moveaxis((codes * scale).reshape(v.shape), -1, axis)


WIDE = False


def mx_kscale(k):
    if not WIDE:
        return np.ones(k)
    levels = np.array([10, -10, 5, -5, 0])
    if k % 512:
        return np.exp2(np.random.permutation(np.resize(levels, k // 32))).repeat(32)
    a = np.empty((k // 512, 16))
    for p in range(k // 512):
        a[p, :8] = np.random.permutation(np.resize(levels, 8))
        for g in range(8):
            far = levels[np.abs(levels - a[p, g]) >= 10]
            a[p, g + 8] = far[np.random.randint(len(far))]
    return np.exp2(a.ravel()).repeat(32)


def f64(x):
    return np.asarray(x).astype(np.float64)


def striped(idx):
    return np.tile(idx.reshape(-1, 16).T, (8, 1)).astype(np.uint16)


def unstriped(offs):
    return offs[:16].T.reshape(-1).astype(np.int64)


E2M1 = np.array([0.0, 0.5, 1.0, 1.5, 2.0, 3.0, 4.0, 6.0, -0.0, -0.5, -1.0, -1.5, -2.0, -3.0, -4.0, -6.0])


def pack_weight(w, fmt):
    k, n = w.shape
    w = f64(np.asarray(w, np.float32).astype(ml_dtypes.bfloat16)).reshape(k // 32, 32, n)
    amax = np.abs(w).max(1)
    if fmt == "e4m3":
        byte = np.frexp(amax)[1] - 1 + 127 - 7
    else:
        mant, ex = np.frexp(amax / 6.0)
        byte = np.where(mant > 0.5, ex, ex - 1) + 127
    byte = np.clip(np.where(amax > 0, byte, 1), 1, 254)
    scaled = (w * np.exp2(127.0 - byte)[:, None, :]).reshape(k, n).astype(np.float32)
    by_word = np.ascontiguousarray(scaled.reshape(k // 512, 128, 4, n).transpose(0, 1, 3, 2))
    if fmt == "e4m3":
        words = by_word.astype(ml_dtypes.float8_e4m3fn).view(np.uint8)
    else:
        c = by_word.astype(ml_dtypes.float4_e2m1fn).view(np.uint8) & 0xF
        words = (c[..., 0::2] | (c[..., 1::2] << 4)).reshape(k // 512, 128, 2 * n)
    return np.ascontiguousarray(words), np.ascontiguousarray(byte.astype(np.uint8).reshape(k // 512, 16, n))


def unpack_weight(words, scales, fmt):
    g, _, n = scales.shape
    words = np.ascontiguousarray(words).reshape(g, 128, n, -1)
    if fmt == "e4m3":
        vals = words.view(ml_dtypes.float8_e4m3fn).astype(np.float64)
    else:
        nib = np.empty((g, 128, n, 4), np.uint8)
        nib[..., 0::2] = words & 0xF
        nib[..., 1::2] = words >> 4
        vals = E2M1[nib]
    vals = vals * np.repeat(np.exp2(scales.astype(np.float64) - 127.0), 8, axis=1)[..., None]
    return vals.transpose(0, 1, 3, 2).reshape(g * 512, n)


K, T, E, C, N = 1024, 1024, 6, 128, 384
K8 = 512


def by_expert(wq, xq):
    return np.concatenate([wq[e].T @ xq[:, e * C:(e + 1) * C] for e in range(E)], axis=1)


def setup_inputs():
    n = np.random.standard_normal
    s = mx_kscale(K)[:, None]
    w = n((E, K, N)) / np.sqrt(K) / s[None]
    w8 = [pack_weight(m[:K8], "e4m3") for m in w]
    w4 = [pack_weight(m[K8:], "e2m1") for m in w]
    return {
        "xT": (n((K, T)) * s).astype(np.float32),
        "w8_words": np.stack([m[0] for m in w8]),
        "w8_scales": np.stack([m[1] for m in w8]),
        "w4_words": np.stack([m[0] for m in w4]),
        "w4_scales": np.stack([m[1] for m in w4]),
        "gate": np.tile(np.random.uniform(0.2, 1.0, E * C), (N, 1)).astype(np.float32),
        "offs": striped(np.random.permutation(T)[:E * C]),
    }


def reference(xT, w8_words, w8_scales, w4_words, w4_scales, gate, offs):
    idx = unstriped(offs)
    w = np.stack([np.concatenate([unpack_weight(w8_words[e], w8_scales[e], "e4m3"), unpack_weight(w4_words[e], w4_scales[e], "e2m1")]) for e in range(E)])
    xq = mxq(f64(xT)[:, idx], 0, "e4m3")
    y = by_expert(w, xq)
    out = np.zeros((N, T))
    out[:, idx] = f64(gate) * y
    return out

@@ -1,0 +1,181 @@
+from contextlib import ExitStack
+
+import concourse.mybir as mybir
+
+F32 = mybir.dt.float32
+BF16 = mybir.dt.bfloat16
+I32 = mybir.dt.int32
+U32 = mybir.dt.uint32
+U16 = mybir.dt.uint16
+U8 = mybir.dt.uint8
+FP8X4 = mybir.dt.float8_e4m3fn_x4
+FP4X4 = mybir.dt.float4_e2m1fn_x4
+MULT = mybir.AluOpType.mult
+
+P = 128
+PACK = 4
+K_PASS = P * PACK
+K, T, E, C, N = 1024, 1024, 6, 128, 384
+S = E * C
+N_BLOCKS = N // P
+PASSES = K // K_PASS
+RUNS = [(0, 2), (2, 6)]
+ROWS = [4, 0]
+
+FLOPS = 2 * S * K * N
+BYTES = 4 * K * T + E * N * (4 * P + 2 * P + 2 * 16) + 4 * S + 2 * S + 4 * N * T
+
+CHUNKS = [(0, 0, 512, 192), (0, 512, 512, 192), (1, 0, 512, 320), (1, 512, 256, 256), (1, 768, 256, 96)]
+
+
+def tile_moe_pln_lin_none_kernel(tc, xT, w8_words, w8_scales, w4_words, w4_scales, gate, offs, out):
+    nc = tc.nc
+    with ExitStack() as ctx:
+        keep = ctx.enter_context(tc.tile_pool(name="keep", bufs=1))
+        psum = ctx.enter_context(tc.psum_pool(name="psum", bufs=1))
+
+        offsets = keep.tile([P, S // 16], U16, name="offsets")
+
+        raws = []
+        groups = []
+        for i, (a, t0, width, unused) in enumerate(CHUNKS):
+            raws.append(keep.tile([P, PACK, width], F32, name="raw%d" % i))
+            groups.append(keep.tile([P, width, PACK], BF16, name="grouped%d" % i, align_bytes=64))
+
+        def load_tokens(i):
+            a, t0, width, unused = CHUNKS[i]
+            rows = xT[a * K_PASS : (a + 1) * K_PASS, t0 : t0 + width]
+            nc.sync.dma_start(out=raws[i][:], in_=rows.rearrange("(p j) t -> p j t", j=PACK))
+
+        load_tokens(0)
+        load_tokens(1)
+        nc.sync.dma_start(offsets[:], offs)
+        for i in range(2, len(CHUNKS)):
+            load_tokens(i)
+
+        token_words, slot_words = [], []
+        for a in range(PASSES):
+            token_words.append(keep.tile([P, T], U32, name="token_words%d" % a, align_bytes=64))
+            slot_words.append(keep.tile([P, S], U32, name="slot_words%d" % a, align_bytes=64))
+        token_bytes = keep.tile([P, T], U8, name="token_bytes", align_bytes=64)
+        slot_bytes = keep.tile([P, S], U8, name="slot_bytes", align_bytes=64)
+        nc.gpsimd.memset(token_bytes[:].bitcast(I32), 0)
+
+        w8 = keep.tile([P, E, 4 * N], U8, name="w8", align_bytes=64)
+        w4 = keep.tile([P, E, 2 * N], U8, name="w4", align_bytes=64)
+        w8_plane = keep.tile([P, E, N], U8, name="w8_plane", align_bytes=64)
+        w4_plane = keep.tile([P, E, N], U8, name="w4_plane", align_bytes=64)
+        for plane in (w8_plane, w4_plane):
+            nc.gpsimd.memset(plane[:].rearrange("p e n -> p (e n)").bitcast(I32), 0)
+
+        windows = []
+        for m in range(N_BLOCKS):
+            windows.append(keep.tile([P, T], F32, name="window%d" % m))
+            nc.vector.memset(windows[m][:], 0.0)
+
+        gates = keep.tile([P, S], F32, name="gates")
+
+        def load_scales(plane, scales, row):
+            for q in range(4):
+                nc.sync.dma_start(
+                    out=plane[32 * q + row : 32 * q + row + 4, :, :].bitcast(I32),
+                    in_=scales[:, 0, 4 * q : 4 * q + 4, :].rearrange("e q n -> q e n").bitcast(I32),
+                )
+
+        def load_w8(run):
+            es = slice(run[0], run[1])
+            nc.sync.dma_start(out=w8[:, es, :].bitcast(I32), in_=w8_words[es, 0].rearrange("e p n r -> p e (n r)").bitcast(I32))
+
+        def load_w4(run):
+            es = slice(run[0], run[1])
+            nc.sync.dma_start(out=w4[:, es, :].bitcast(I32), in_=w4_words[es, 0].rearrange("e p b -> p e b").bitcast(I32))
+
+        load_scales(w8_plane, w8_scales, ROWS[0])
+        load_w8(RUNS[0])
+        load_scales(w4_plane, w4_scales, ROWS[1])
+        load_w4(RUNS[0])
+        nc.sync.dma_start(out=gates[:], in_=gate[0:P, :])
+        load_w8(RUNS[1])
+        load_w4(RUNS[1])
+
+        def interleave(i):
+            width, share = CHUNKS[i][2:]
+            for engine, cols in ((nc.scalar.copy, slice(0, share)), (nc.vector.tensor_copy, slice(share, width))):
+                if cols.start == cols.stop:
+                    continue
+                engine(
+                    out=groups[i][:, cols, :].rearrange("p (c i) j -> p c j i", i=4),
+                    in_=raws[i][:, :, cols].rearrange("p j (c i) -> p c j i", i=4),
+                )
+
+        def quantise(i):
+            a, t0, width, unused = CHUNKS[i]
+            nc.vector.quantize_mx(
+                out=token_words[a][:, t0 : t0 + width].bitcast(FP8X4),
+                scales=token_bytes[ROWS[a] :, t0 : t0 + width],
+                in_=groups[i][:].rearrange("p t j -> p (t j)"),
+            )
+
+        def gather(tokens, slots, s0, s1):
+            nc.vector.tensor_copy(slots[:, s0:s1], tokens[:].indirect(offsets[:, s0 // 16 : s1 // 16]))
+
+        interleave(0)
+        quantise(0)
+        interleave(1)
+        quantise(1)
+        gather(token_words[0], slot_words[0], 0, S)
+        interleave(2)
+        interleave(3)
+        quantise(2)
+        interleave(4)
+        quantise(3)
+        quantise(4)
+        for e0, e1 in RUNS:
+            gather(token_words[1], slot_words[1], e0 * C, e1 * C)
+            gather(token_bytes, slot_bytes, e0 * C, e1 * C)
+
+        results = []
+        for m in range(N_BLOCKS):
+            results.append(keep.tile([P, S], F32, name="result%d" % m))
+
+        def multiply(run, m):
+            e0, e1 = run
+            acc = psum.tile([P, (e1 - e0) * C], F32, name="acc%d_%d" % (e0, m))
+            for e in range(e0, e1):
+                i = e - e0
+                cols = slice(e * C, (e + 1) * C)
+                for a in range(PASSES):
+                    if a == 0:
+                        codes = w8[:, e, 4 * P * m : 4 * P * (m + 1)].bitcast(FP8X4)
+                        plane = w8_plane
+                    else:
+                        codes = w4[:, e, 2 * P * m : 2 * P * (m + 1)].bitcast(FP4X4)
+                        plane = w4_plane
+                    nc.tensor.matmul_mx(
+                        out=acc[:, i * C : (i + 1) * C],
+                        lhsT=codes,
+                        lhsT_scale=plane[ROWS[a] :, e, P * m : P * (m + 1)],
+                        rhs=slot_words[a][:, cols].bitcast(FP8X4),
+                        rhs_scale=slot_bytes[ROWS[a] :, cols],
+                        start=(a == 0),
+                        stop=(a == PASSES - 1),
+                    )
+            nc.scalar.copy(out=results[m][:, e0 * C : e1 * C], in_=acc[:])
+
+        for run in RUNS:
+            for m in range(N_BLOCKS):
+                multiply(run, m)
+
+        def scatter(m, s0, s1):
+            nc.vector.tensor_tensor(
+                windows[m][:].indirect(offsets[:, s0 // 16 : s1 // 16]),
+                results[m][:, s0:s1],
+                gates[:, s0:s1],
+                MULT,
+            )
+
+        for e0, e1 in RUNS:
+            for m in range(N_BLOCKS):
+                scatter(m, e0 * C, e1 * C)
+        for m in range(N_BLOCKS):
+            nc.sync.dma_start(out=out[m * P : (m + 1) * P, :], in_=windows[m][:])

@@ -19,13 +19,15 @@ K, T, E, C, N = 1024, 1024, 6, 128, 384
 S = E * C
 N_BLOCKS = N // P
 PASSES = K // K_PASS
+GROUP = 256
+GROUPS = S // GROUP
+W8_ROW = 4
 RUNS = [(0, 2), (2, 6)]
-ROWS = [4, 0]
 
 FLOPS = 2 * S * K * N
 BYTES = 4 * K * T + E * N * (4 * P + 2 * P + 2 * 16) + 4 * S + 2 * S + 4 * N * T
 
-CHUNKS = [(0, 0, 512, 192), (0, 512, 512, 192), (1, 0, 512, 320), (1, 512, 256, 256), (1, 768, 256, 96)]
+LOADS = [(0, 0, 1024, 384), (1, 0, 1024, 576), (2, 0, 1024, 576), (3, 0, 512, 288), (3, 512, 512, 288)]
 
 
 def tile_moe_pln_lin_none_kernel(tc, xT, w8_words, w8_scales, w4_words, w4_scales, gate, offs, out):
@@ -37,102 +39,102 @@ def tile_moe_pln_lin_none_kernel(tc, xT, w8_words, w8_scales, w4_words, w4_scale
         offsets = keep.tile([P, S // 16], U16, name="offsets")
 
         raws = []
-        groups = []
-        for i, (a, t0, width, unused) in enumerate(CHUNKS):
-            raws.append(keep.tile([P, PACK, width], F32, name="raw%d" % i))
-            groups.append(keep.tile([P, width, PACK], BF16, name="grouped%d" % i, align_bytes=64))
+        for i, (pair, t0, width, unused) in enumerate(LOADS):
+            a, u = divmod(pair, 2)
+            raws.append(keep.tile([P, 2, width], F32, name="raw%d" % i, tag="raw%d" % i, align_bytes=64))
+            rows = xT[a * K_PASS : (a + 1) * K_PASS, t0 : t0 + width].rearrange("(p j) t -> p j t", j=PACK)
+            nc.sync.dma_start(out=raws[i][:], in_=rows[:, 2 * u : 2 * u + 2, :])
+            if i == 0:
+                nc.sync.dma_start(offsets[:], offs)
 
-        def load_tokens(i):
-            a, t0, width, unused = CHUNKS[i]
-            rows = xT[a * K_PASS : (a + 1) * K_PASS, t0 : t0 + width]
-            nc.sync.dma_start(out=raws[i][:], in_=rows.rearrange("(p j) t -> p j t", j=PACK))
-
-        load_tokens(0)
-        load_tokens(1)
-        nc.sync.dma_start(offsets[:], offs)
-        for i in range(2, len(CHUNKS)):
-            load_tokens(i)
-
-        token_words, slot_words = [], []
-        for a in range(PASSES):
-            token_words.append(keep.tile([P, T], U32, name="token_words%d" % a, align_bytes=64))
-            slot_words.append(keep.tile([P, S], U32, name="slot_words%d" % a, align_bytes=64))
-        token_bytes = keep.tile([P, T], U8, name="token_bytes", align_bytes=64)
-        slot_bytes = keep.tile([P, S], U8, name="slot_bytes", align_bytes=64)
-        nc.gpsimd.memset(token_bytes[:].bitcast(I32), 0)
+        pairs = []
+        for pair in range(4):
+            pairs.append(keep.tile([P, T], U32, name="pair%d" % pair, align_bytes=64))
+        picked = keep.tile([P, 4 * GROUPS, GROUP], U32, name="picked", align_bytes=64)
+        codes = keep.tile([P, GROUPS, PASSES * GROUP], U32, name="codes", align_bytes=64)
+        plane = keep.tile([P, GROUPS, PASSES * GROUP], U8, name="plane", align_bytes=64)
+        nc.gpsimd.memset(plane[:].rearrange("p g n -> p (g n)").bitcast(I32), 0)
 
         w8 = keep.tile([P, E, 4 * N], U8, name="w8", align_bytes=64)
         w4 = keep.tile([P, E, 2 * N], U8, name="w4", align_bytes=64)
         w8_plane = keep.tile([P, E, N], U8, name="w8_plane", align_bytes=64)
         w4_plane = keep.tile([P, E, N], U8, name="w4_plane", align_bytes=64)
-        for plane in (w8_plane, w4_plane):
-            nc.gpsimd.memset(plane[:].rearrange("p e n -> p (e n)").bitcast(I32), 0)
+        for w_plane in (w8_plane, w4_plane):
+            nc.gpsimd.memset(w_plane[:].rearrange("p e n -> p (e n)").bitcast(I32), 0)
 
         windows = []
         for m in range(N_BLOCKS):
             windows.append(keep.tile([P, T], F32, name="window%d" % m))
-            nc.vector.memset(windows[m][:], 0.0)
+            if m < N_BLOCKS - 1:
+                nc.vector.memset(windows[m][:], 0.0)
+            else:
+                nc.scalar.copy(out=windows[m][:], in_=windows[0][:])
 
         gates = keep.tile([P, S], F32, name="gates")
 
-        def load_scales(plane, scales, row):
-            for q in range(4):
-                nc.sync.dma_start(
-                    out=plane[32 * q + row : 32 * q + row + 4, :, :].bitcast(I32),
-                    in_=scales[:, 0, 4 * q : 4 * q + 4, :].rearrange("e q n -> q e n").bitcast(I32),
-                )
-
-        def load_w8(run):
-            es = slice(run[0], run[1])
-            nc.sync.dma_start(out=w8[:, es, :].bitcast(I32), in_=w8_words[es, 0].rearrange("e p n r -> p e (n r)").bitcast(I32))
-
-        def load_w4(run):
-            es = slice(run[0], run[1])
-            nc.sync.dma_start(out=w4[:, es, :].bitcast(I32), in_=w4_words[es, 0].rearrange("e p b -> p e b").bitcast(I32))
-
-        load_scales(w8_plane, w8_scales, ROWS[0])
-        load_w8(RUNS[0])
-        load_scales(w4_plane, w4_scales, ROWS[1])
-        load_w4(RUNS[0])
-        nc.sync.dma_start(out=gates[:], in_=gate[0:P, :])
-        load_w8(RUNS[1])
-        load_w4(RUNS[1])
-
-        def interleave(i):
-            width, share = CHUNKS[i][2:]
-            for engine, cols in ((nc.scalar.copy, slice(0, share)), (nc.vector.tensor_copy, slice(share, width))):
-                if cols.start == cols.stop:
-                    continue
-                engine(
-                    out=groups[i][:, cols, :].rearrange("p (c i) j -> p c j i", i=4),
-                    in_=raws[i][:, :, cols].rearrange("p j (c i) -> p c j i", i=4),
-                )
-
-        def quantise(i):
-            a, t0, width, unused = CHUNKS[i]
-            nc.vector.quantize_mx(
-                out=token_words[a][:, t0 : t0 + width].bitcast(FP8X4),
-                scales=token_bytes[ROWS[a] :, t0 : t0 + width],
-                in_=groups[i][:].rearrange("p t j -> p (t j)"),
+        def load_scales(w_plane, scales, row, r):
+            nc.sync.dma_start(
+                out=w_plane[row + r : P : 32, :, :].bitcast(I32),
+                in_=scales[:, 0, r:16:4, :].rearrange("e q n -> q e n").bitcast(I32),
             )
 
-        def gather(tokens, slots, s0, s1):
-            nc.vector.tensor_copy(slots[:, s0:s1], tokens[:].indirect(offsets[:, s0 // 16 : s1 // 16]))
+        def load_weights(run):
+            es = slice(run[0], run[1])
+            nc.sync.dma_start(out=w8[:, es, :].bitcast(I32), in_=w8_words[es, 0].rearrange("e p n r -> p e (n r)").bitcast(I32))
+            nc.sync.dma_start(out=w4[:, es, :].bitcast(I32), in_=w4_words[es, 0].rearrange("e p b -> p e b").bitcast(I32))
 
-        interleave(0)
-        quantise(0)
-        interleave(1)
-        quantise(1)
-        gather(token_words[0], slot_words[0], 0, S)
-        interleave(2)
-        interleave(3)
-        quantise(2)
-        interleave(4)
-        quantise(3)
-        quantise(4)
-        for e0, e1 in RUNS:
-            gather(token_words[1], slot_words[1], e0 * C, e1 * C)
-            gather(token_bytes, slot_bytes, e0 * C, e1 * C)
+        load_weights(RUNS[0])
+        for r in range(4):
+            load_scales(w8_plane, w8_scales, W8_ROW, r)
+            load_scales(w4_plane, w4_scales, 0, r)
+        nc.sync.dma_start(out=gates[:], in_=gate[0:P, :])
+        load_weights(RUNS[1])
+
+        def round_pair(i):
+            pair, t0, width, share = LOADS[i]
+            halves = pairs[pair][:, t0 : t0 + width].bitcast(BF16).rearrange("p (t e) -> p t e", e=2)
+            first, rest = slice(0, share), slice(share, width)
+            nc.scalar.copy(
+                out=halves[:, first, :].rearrange("p (c i) e -> p c e i", i=4),
+                in_=raws[i][:, :, first].rearrange("p e (c i) -> p c e i", i=4),
+            )
+            if i == 0:
+                nc.vector.tensor_copy(
+                    out=halves[:, rest, :].rearrange("p (c i) e -> p c e i", i=4),
+                    in_=raws[i][:, :, rest].rearrange("p e (c i) -> p c e i", i=4),
+                )
+            else:
+                nc.gpsimd.tensor_copy(out=halves[:, rest, :], in_=raws[i][:, :, rest].rearrange("p e t -> p t e"))
+
+        def gather(pair, g0, g1, block):
+            nc.vector.tensor_copy(
+                picked[:, block : block + g1 - g0, :].rearrange("p b s -> p (b s)"),
+                pairs[pair][:].indirect(offsets[:, g0 * GROUP // 16 : g1 * GROUP // 16]),
+            )
+
+        round_pair(0)
+        gather(0, 0, 3, 0)
+        round_pair(1)
+        gather(1, 0, 3, 3)
+        round_pair(2)
+        gather(2, 0, 3, 6)
+        round_pair(3)
+        round_pair(4)
+        for g in range(GROUPS):
+            gather(3, g, g + 1, 9 + g)
+
+        woven = keep.tile([P, GROUPS, PASSES, GROUP, 2], U32, name="woven", tag="raw4", align_bytes=64)
+        for g in range(GROUPS):
+            nc.gpsimd.tensor_copy(out=woven[:, g, 0], in_=picked[:, g : g + 4 : 3, :].rearrange("p u s -> p s u"))
+            nc.scalar.copy(
+                out=woven[:, g, 1].rearrange("p (c i) u -> p c u i", i=4),
+                in_=picked[:, 6 + g : 12 : 3, :].rearrange("p u (c i) -> p c u i", i=4),
+            )
+            nc.vector.quantize_mx(
+                out=codes[:, g, :].bitcast(FP8X4),
+                scales=plane[:, g, :],
+                in_=woven[:, g].rearrange("p a s u -> p (a s u)").bitcast(BF16),
+            )
 
         results = []
         for m in range(N_BLOCKS):
@@ -142,21 +144,21 @@ def tile_moe_pln_lin_none_kernel(tc, xT, w8_words, w8_scales, w4_words, w4_scale
             e0, e1 = run
             acc = psum.tile([P, (e1 - e0) * C], F32, name="acc%d_%d" % (e0, m))
             for e in range(e0, e1):
-                i = e - e0
-                cols = slice(e * C, (e + 1) * C)
+                g, i = divmod(e, 2)
                 for a in range(PASSES):
+                    cols = slice(a * GROUP + i * C, a * GROUP + (i + 1) * C)
                     if a == 0:
-                        codes = w8[:, e, 4 * P * m : 4 * P * (m + 1)].bitcast(FP8X4)
-                        plane = w8_plane
+                        w_codes = w8[:, e, 4 * P * m : 4 * P * (m + 1)].bitcast(FP8X4)
+                        w_scale = w8_plane[W8_ROW:, e, P * m : P * (m + 1)]
                     else:
-                        codes = w4[:, e, 2 * P * m : 2 * P * (m + 1)].bitcast(FP4X4)
-                        plane = w4_plane
+                        w_codes = w4[:, e, 2 * P * m : 2 * P * (m + 1)].bitcast(FP4X4)
+                        w_scale = w4_plane[:, e, P * m : P * (m + 1)]
                     nc.tensor.matmul_mx(
-                        out=acc[:, i * C : (i + 1) * C],
-                        lhsT=codes,
-                        lhsT_scale=plane[ROWS[a] :, e, P * m : P * (m + 1)],
-                        rhs=slot_words[a][:, cols].bitcast(FP8X4),
-                        rhs_scale=slot_bytes[ROWS[a] :, cols],
+                        out=acc[:, (e - e0) * C : (e - e0 + 1) * C],
+                        lhsT=w_codes,
+                        lhsT_scale=w_scale,
+                        rhs=codes[:, g, cols].bitcast(FP8X4),
+                        rhs_scale=plane[:, g, cols],
                         start=(a == 0),
                         stop=(a == PASSES - 1),
                     )
@@ -166,16 +168,13 @@ def tile_moe_pln_lin_none_kernel(tc, xT, w8_words, w8_scales, w4_words, w4_scale
             for m in range(N_BLOCKS):
                 multiply(run, m)
 
-        def scatter(m, s0, s1):
-            nc.vector.tensor_tensor(
-                windows[m][:].indirect(offsets[:, s0 // 16 : s1 // 16]),
-                results[m][:, s0:s1],
-                gates[:, s0:s1],
-                MULT,
-            )
-
         for e0, e1 in RUNS:
             for m in range(N_BLOCKS):
-                scatter(m, e0 * C, e1 * C)
+                nc.vector.tensor_tensor(
+                    windows[m][:].indirect(offsets[:, e0 * C // 16 : e1 * C // 16]),
+                    results[m][:, e0 * C : e1 * C],
+                    gates[:, e0 * C : e1 * C],
+                    MULT,
+                )
         for m in range(N_BLOCKS):
             nc.sync.dma_start(out=out[m * P : (m + 1) * P, :], in_=windows[m][:])

@@ -27,13 +27,14 @@ RUNS = [(0, 2), (2, 6)]
 FLOPS = 2 * S * K * N
 BYTES = 4 * K * T + E * N * (4 * P + 2 * P + 2 * 16) + 4 * S + 2 * S + 4 * N * T
 
-LOADS = [(0, 0, 1024, 384), (1, 0, 1024, 576), (2, 0, 1024, 576), (3, 0, 512, 288), (3, 512, 512, 288)]
+LOADS = [(0, 0, 1024, 384), (1, 0, 1024, 576), (2, 0, 1024, 576), (3, 0, 512, 288), (3, 512, 512, 272)]
 
 
 def tile_moe_pln_lin_none_kernel(tc, xT, w8_words, w8_scales, w4_words, w4_scales, gate, offs, out):
     nc = tc.nc
     with ExitStack() as ctx:
         keep = ctx.enter_context(tc.tile_pool(name="keep", bufs=1))
+        shared = ctx.enter_context(tc.tile_pool(name="shared", bufs=1))
         psum = ctx.enter_context(tc.psum_pool(name="psum", bufs=1))
 
         offsets = keep.tile([P, S // 16], U16, name="offsets")
@@ -41,9 +42,13 @@ def tile_moe_pln_lin_none_kernel(tc, xT, w8_words, w8_scales, w4_words, w4_scale
         raws = []
         for i, (pair, t0, width, unused) in enumerate(LOADS):
             a, u = divmod(pair, 2)
-            raws.append(keep.tile([P, 2, width], F32, name="raw%d" % i, tag="raw%d" % i, align_bytes=64))
+            if i < len(LOADS) - 1:
+                raws.append(keep.tile([P, 2, width], F32, name="raw%d" % i)[:])
+            else:
+                room = shared.tile([P, 2 * GROUPS, width], F32, name="raw%d" % i, offset=0, align_bytes=64)
+                raws.append(room[:, 0:2, :])
             rows = xT[a * K_PASS : (a + 1) * K_PASS, t0 : t0 + width].rearrange("(p j) t -> p j t", j=PACK)
-            nc.sync.dma_start(out=raws[i][:], in_=rows[:, 2 * u : 2 * u + 2, :])
+            nc.sync.dma_start(out=raws[i], in_=rows[:, 2 * u : 2 * u + 2, :])
             if i == 0:
                 nc.sync.dma_start(offsets[:], offs)
 
@@ -83,10 +88,11 @@ def tile_moe_pln_lin_none_kernel(tc, xT, w8_words, w8_scales, w4_words, w4_scale
             nc.sync.dma_start(out=w8[:, es, :].bitcast(I32), in_=w8_words[es, 0].rearrange("e p n r -> p e (n r)").bitcast(I32))
             nc.sync.dma_start(out=w4[:, es, :].bitcast(I32), in_=w4_words[es, 0].rearrange("e p b -> p e b").bitcast(I32))
 
-        load_weights(RUNS[0])
         for r in range(4):
             load_scales(w8_plane, w8_scales, W8_ROW, r)
             load_scales(w4_plane, w4_scales, 0, r)
+            if r == 0:
+                load_weights(RUNS[0])
         nc.sync.dma_start(out=gates[:], in_=gate[0:P, :])
         load_weights(RUNS[1])
 
@@ -120,21 +126,38 @@ def tile_moe_pln_lin_none_kernel(tc, xT, w8_words, w8_scales, w4_words, w4_scale
         gather(2, 0, 3, 6)
         round_pair(3)
         round_pair(4)
+
+        woven = []
+        for g in range(GROUPS):
+            woven.append(shared.tile([P, 2, PASSES, C, 2], U32, name="woven%d" % g, offset=g * PASSES * GROUP * 8, align_bytes=64))
+
+        def weave(g, a, on_scalar):
+            two = picked[:, 6 * a + g : 6 * a + 6 : 3, :]
+            if on_scalar:
+                nc.scalar.copy(
+                    out=woven[g][:, :, a].rearrange("p e (c i) u -> p e c u i", i=4),
+                    in_=two.rearrange("p u (e c i) -> p e c u i", e=2, i=4),
+                )
+            else:
+                nc.gpsimd.tensor_copy(out=woven[g][:, :, a], in_=two.rearrange("p u (e s) -> p e s u", e=2))
+
+        def quantise(e0, e1):
+            g, i = divmod(e0, 2)
+            cols = slice(i * PASSES * C, (i + e1 - e0) * PASSES * C)
+            nc.vector.quantize_mx(
+                out=codes[:, g, cols].bitcast(FP8X4),
+                scales=plane[:, g, cols],
+                in_=woven[g][:, i : i + e1 - e0].rearrange("p e a s u -> p (e a s u)").bitcast(BF16),
+            )
+
         for g in range(GROUPS):
             gather(3, g, g + 1, 9 + g)
-
-        woven = keep.tile([P, GROUPS, PASSES, GROUP, 2], U32, name="woven", tag="raw4", align_bytes=64)
         for g in range(GROUPS):
-            nc.gpsimd.tensor_copy(out=woven[:, g, 0], in_=picked[:, g : g + 4 : 3, :].rearrange("p u s -> p s u"))
-            nc.scalar.copy(
-                out=woven[:, g, 1].rearrange("p (c i) u -> p c u i", i=4),
-                in_=picked[:, 6 + g : 12 : 3, :].rearrange("p u (c i) -> p c u i", i=4),
-            )
-            nc.vector.quantize_mx(
-                out=codes[:, g, :].bitcast(FP8X4),
-                scales=plane[:, g, :],
-                in_=woven[:, g].rearrange("p a s u -> p (a s u)").bitcast(BF16),
-            )
+            weave(g, 0, g < GROUPS - 1)
+        for g in range(GROUPS):
+            weave(g, 1, g > 0)
+        for e0, e1 in ((0, 1), (1, 2), (2, 4), (4, 6)):
+            quantise(e0, e1)
 
         results = []
         for m in range(N_BLOCKS):
@@ -146,7 +169,7 @@ def tile_moe_pln_lin_none_kernel(tc, xT, w8_words, w8_scales, w4_words, w4_scale
             for e in range(e0, e1):
                 g, i = divmod(e, 2)
                 for a in range(PASSES):
-                    cols = slice(a * GROUP + i * C, a * GROUP + (i + 1) * C)
+                    cols = slice((i * PASSES + a) * C, (i * PASSES + a + 1) * C)
                     if a == 0:
                         w_codes = w8[:, e, 4 * P * m : 4 * P * (m + 1)].bitcast(FP8X4)
                         w_scale = w8_plane[W8_ROW:, e, P * m : P * (m + 1)]
@@ -164,9 +187,12 @@ def tile_moe_pln_lin_none_kernel(tc, xT, w8_words, w8_scales, w4_words, w4_scale
                     )
             nc.scalar.copy(out=results[m][:, e0 * C : e1 * C], in_=acc[:])
 
+        multiply((0, 1), 0)
+        multiply((1, 2), 0)
         for run in RUNS:
             for m in range(N_BLOCKS):
-                multiply(run, m)
+                if (run, m) != (RUNS[0], 0):
+                    multiply(run, m)
 
         for e0, e1 in RUNS:
             for m in range(N_BLOCKS):

@@ -27,7 +27,7 @@ RUNS = [(0, 2), (2, 6)]
 FLOPS = 2 * S * K * N
 BYTES = 4 * K * T + E * N * (4 * P + 2 * P + 2 * 16) + 4 * S + 2 * S + 4 * N * T
 
-LOADS = [(0, 0, 1024, 384), (1, 0, 1024, 576), (2, 0, 1024, 576), (3, 0, 512, 288), (3, 512, 512, 272)]
+LOADS = [(0, 0, 1024, 384), (1, 0, 1024, 512), (2, 0, 1024, 512), (3, 0, 512, 256), (3, 512, 512, 256)]
 
 
 def tile_moe_pln_lin_none_kernel(tc, xT, w8_words, w8_scales, w4_words, w4_scales, gate, offs, out):
@@ -58,7 +58,6 @@ def tile_moe_pln_lin_none_kernel(tc, xT, w8_words, w8_scales, w4_words, w4_scale
         picked = keep.tile([P, 4 * GROUPS, GROUP], U32, name="picked", align_bytes=64)
         codes = keep.tile([P, GROUPS, PASSES * GROUP], U32, name="codes", align_bytes=64)
         plane = keep.tile([P, GROUPS, PASSES * GROUP], U8, name="plane", align_bytes=64)
-        nc.gpsimd.memset(plane[:].rearrange("p g n -> p (g n)").bitcast(I32), 0)
 
         w8 = keep.tile([P, E, 4 * N], U8, name="w8", align_bytes=64)
         w4 = keep.tile([P, E, 2 * N], U8, name="w4", align_bytes=64)
@@ -187,20 +186,16 @@ def tile_moe_pln_lin_none_kernel(tc, xT, w8_words, w8_scales, w4_words, w4_scale
                     )
             nc.scalar.copy(out=results[m][:, e0 * C : e1 * C], in_=acc[:])
 
-        multiply((0, 1), 0)
-        multiply((1, 2), 0)
-        for run in RUNS:
-            for m in range(N_BLOCKS):
-                if (run, m) != (RUNS[0], 0):
-                    multiply(run, m)
+        steps = [((0, 1), 0), ((0, 2), 1), ((1, 2), 0), ((0, 2), 2)] + [(RUNS[1], m) for m in range(N_BLOCKS)]
+        for run, m in steps:
+            multiply(run, m)
 
-        for e0, e1 in RUNS:
-            for m in range(N_BLOCKS):
-                nc.vector.tensor_tensor(
-                    windows[m][:].indirect(offsets[:, e0 * C // 16 : e1 * C // 16]),
-                    results[m][:, e0 * C : e1 * C],
-                    gates[:, e0 * C : e1 * C],
-                    MULT,
-                )
+        for (e0, e1), m in steps:
+            nc.vector.tensor_tensor(
+                windows[m][:].indirect(offsets[:, e0 * C // 16 : e1 * C // 16]),
+                results[m][:, e0 * C : e1 * C],
+                gates[:, e0 * C : e1 * C],
+                MULT,
+            )
         for m in range(N_BLOCKS):
             nc.sync.dma_start(out=out[m * P : (m + 1) * P, :], in_=windows[m][:])

@@ -11,6 +11,7 @@ U8 = mybir.dt.uint8
 FP8X4 = mybir.dt.float8_e4m3fn_x4
 FP4X4 = mybir.dt.float4_e2m1fn_x4
 MULT = mybir.AluOpType.mult
+COPY = mybir.ActivationFunctionType.Copy
 
 P = 128
 PACK = 4
@@ -19,10 +20,8 @@ K, T, E, C, N = 1024, 1024, 6, 128, 384
 S = E * C
 N_BLOCKS = N // P
 PASSES = K // K_PASS
-GROUP = 256
-GROUPS = S // GROUP
-W8_ROW = 4
-RUNS = [(0, 2), (2, 6)]
+PAIRS = 4
+GROUPS = [(0, 1), (1, 3), (3, 6)]
 
 FLOPS = 2 * S * K * N
 BYTES = 4 * K * T + E * N * (4 * P + 2 * P + 2 * 16) + 4 * S + 2 * S + 4 * N * T
@@ -39,32 +38,73 @@ def tile_moe_pln_lin_none_kernel(tc, xT, w8_words, w8_scales, w4_words, w4_scale
 
         offsets = keep.tile([P, S // 16], U16, name="offsets")
 
+        def listed(e0, e1):
+            return offsets[:, e0 * C // 16 : e1 * C // 16]
+
         raws = []
         for i, (pair, t0, width, unused) in enumerate(LOADS):
-            a, u = divmod(pair, 2)
-            if i < len(LOADS) - 1:
-                raws.append(keep.tile([P, 2, width], F32, name="raw%d" % i)[:])
+            if i < 3:
+                raws.append(keep.tile([P, 2, width], F32, name="raw%d" % i))
             else:
-                room = shared.tile([P, 2 * GROUPS, width], F32, name="raw%d" % i, offset=0, align_bytes=64)
-                raws.append(room[:, 0:2, :])
+                raws.append(shared.tile([P, 2, width], F32, name="raw%d" % i, offset=1024 + (i - 3) * 7168, align_bytes=64))
+
+        def load_x(i):
+            pair, t0, width, unused = LOADS[i]
+            a, u = divmod(pair, 2)
             rows = xT[a * K_PASS : (a + 1) * K_PASS, t0 : t0 + width].rearrange("(p j) t -> p j t", j=PACK)
-            nc.sync.dma_start(out=raws[i], in_=rows[:, 2 * u : 2 * u + 2, :])
-            if i == 0:
-                nc.sync.dma_start(offsets[:], offs)
+            nc.sync.dma_start(out=raws[i][:], in_=rows[:, 2 * u : 2 * u + 2, :])
 
-        pairs = []
-        for pair in range(4):
-            pairs.append(keep.tile([P, T], U32, name="pair%d" % pair, align_bytes=64))
-        picked = keep.tile([P, 4 * GROUPS, GROUP], U32, name="picked", align_bytes=64)
-        codes = keep.tile([P, GROUPS, PASSES * GROUP], U32, name="codes", align_bytes=64)
-        plane = keep.tile([P, GROUPS, PASSES * GROUP], U8, name="plane", align_bytes=64)
-
-        w8 = keep.tile([P, E, 4 * N], U8, name="w8", align_bytes=64)
-        w4 = keep.tile([P, E, 2 * N], U8, name="w4", align_bytes=64)
-        w8_plane = keep.tile([P, E, N], U8, name="w8_plane", align_bytes=64)
+        w8, w4, gates = [], [], []
+        for g, (e0, e1) in enumerate(GROUPS):
+            w8.append(keep.tile([P, e1 - e0, 4 * N], U8, name="w8_%d" % g, align_bytes=64))
+            w4.append(keep.tile([P, e1 - e0, 2 * N], U8, name="w4_%d" % g, align_bytes=64))
+        gate_tiles = {}
+        for e0, e1, m, place in [(0, 1, 0, 18176), (1, 3, 0, 24576), (3, 6, 0, 28672)]:
+            gate_tiles[e0] = shared.tile([P, (e1 - e0) * C], F32, name="gate%d" % e0, offset=place, align_bytes=64)[:]
+        w8_planes = [keep.tile([P, N], U8, name="w8_plane%d" % h, align_bytes=64) for h in range(2)]
         w4_plane = keep.tile([P, E, N], U8, name="w4_plane", align_bytes=64)
-        for w_plane in (w8_plane, w4_plane):
-            nc.gpsimd.memset(w_plane[:].rearrange("p e n -> p (e n)").bitcast(I32), 0)
+
+        def w8_row(e):
+            return 4 * e if e < 4 else 4 * e - 8
+
+        def load_w8_scales(h):
+            e0, e1 = (0, 4) if h == 0 else (4, 6)
+            for q in range(4):
+                nc.sync.dma_start(
+                    out=w8_planes[h][32 * q + w8_row(e0) : 32 * q + 16, :].bitcast(I32),
+                    in_=w8_scales[e0:e1, 0, 4 * q : 4 * q + 4, :].bitcast(I32),
+                )
+
+        def load_w4_scales():
+            for r in range(4):
+                nc.sync.dma_start(
+                    out=w4_plane[r:P:32, :, :].bitcast(I32),
+                    in_=w4_scales[:, 0, r:16:4, :].rearrange("e q n -> q e n").bitcast(I32),
+                )
+
+        def load_weights(g):
+            es = slice(GROUPS[g][0], GROUPS[g][1])
+            nc.sync.dma_start(out=w8[g][:].bitcast(I32), in_=w8_words[es, 0].rearrange("e p n r -> p e (n r)").bitcast(I32))
+            nc.sync.dma_start(out=w4[g][:].bitcast(I32), in_=w4_words[es, 0].rearrange("e p b -> p e b").bitcast(I32))
+
+        def load_gate(e0, e1):
+            nc.sync.dma_start(out=gate_tiles[e0], in_=gate[0:P, e0 * C : e1 * C])
+
+        load_x(0)
+        nc.sync.dma_start(offsets[:], offs)
+        load_x(1)
+        load_w8_scales(0)
+        load_x(2)
+        load_x(3)
+        load_x(4)
+        load_gate(0, 1)
+        load_weights(0)
+        load_w4_scales()
+        load_weights(1)
+        load_gate(1, 3)
+        load_weights(2)
+        load_gate(3, 6)
+        load_w8_scales(1)
 
         windows = []
         for m in range(N_BLOCKS):
@@ -74,26 +114,30 @@ def tile_moe_pln_lin_none_kernel(tc, xT, w8_words, w8_scales, w4_words, w4_scale
             else:
                 nc.scalar.copy(out=windows[m][:], in_=windows[0][:])
 
-        gates = keep.tile([P, S], F32, name="gates")
-
-        def load_scales(w_plane, scales, row, r):
-            nc.sync.dma_start(
-                out=w_plane[row + r : P : 32, :, :].bitcast(I32),
-                in_=scales[:, 0, r:16:4, :].rearrange("e q n -> q e n").bitcast(I32),
-            )
-
-        def load_weights(run):
-            es = slice(run[0], run[1])
-            nc.sync.dma_start(out=w8[:, es, :].bitcast(I32), in_=w8_words[es, 0].rearrange("e p n r -> p e (n r)").bitcast(I32))
-            nc.sync.dma_start(out=w4[:, es, :].bitcast(I32), in_=w4_words[es, 0].rearrange("e p b -> p e b").bitcast(I32))
-
-        for r in range(4):
-            load_scales(w8_plane, w8_scales, W8_ROW, r)
-            load_scales(w4_plane, w4_scales, 0, r)
-            if r == 0:
-                load_weights(RUNS[0])
-        nc.sync.dma_start(out=gates[:], in_=gate[0:P, :])
-        load_weights(RUNS[1])
+        pairs = [keep.tile([P, T], U32, name="pair%d" % u, align_bytes=64) for u in range(PAIRS)]
+        picked = keep.tile([P, PAIRS, S], U32, name="picked", align_bytes=64)
+        woven, codes, planes = {}, {}, {}
+        for g, (e0, e1) in enumerate(GROUPS):
+            n = (e1 - e0) * C
+            if g == 0:
+                woven[g, 0] = keep.tile([P, n, 2], U32, name="woven00", align_bytes=64)[:]
+                woven[g, 1] = picked[:, 3, 3 * C : 5 * C].rearrange("p (s u) -> p s u", u=2)
+            elif g == 1:
+                both = shared.tile([P, PASSES, n, 2], U32, name="woven%d" % g, offset=2048, align_bytes=64)
+                woven[g] = both[:]
+                woven[g, 0], woven[g, 1] = both[:, 0], both[:, 1]
+            else:
+                woven[g, 0] = shared.tile([P, n, 2], U32, name="woven20", offset=8192, align_bytes=64)[:]
+                woven[g, 1] = shared.tile([P, n, 2], U32, name="woven21", offset=13312, align_bytes=64)[:]
+            if g == 1:
+                both = shared.tile([P, PASSES * n], U32, name="codes1", offset=16384, align_bytes=64)
+                codes[g], codes[g, 0], codes[g, 1] = both[:], both[:, 0:n], both[:, n : 2 * n]
+            else:
+                for a in range(PASSES):
+                    place = 12288 + 512 * a if g == 0 else (18432, 20480)[a]
+                    codes[g, a] = shared.tile([P, n], U32, name="codes%d%d" % (g, a), offset=place, align_bytes=64)[:]
+            both = keep.tile([P, PASSES * n], U8, name="plane%d" % g, align_bytes=64)
+            planes[g], planes[g, 0], planes[g, 1] = both[:], both[:, 0:n], both[:, n : 2 * n]
 
         def round_pair(i):
             pair, t0, width, share = LOADS[i]
@@ -111,91 +155,114 @@ def tile_moe_pln_lin_none_kernel(tc, xT, w8_words, w8_scales, w4_words, w4_scale
             else:
                 nc.gpsimd.tensor_copy(out=halves[:, rest, :], in_=raws[i][:, :, rest].rearrange("p e t -> p t e"))
 
-        def gather(pair, g0, g1, block):
-            nc.vector.tensor_copy(
-                picked[:, block : block + g1 - g0, :].rearrange("p b s -> p (b s)"),
-                pairs[pair][:].indirect(offsets[:, g0 * GROUP // 16 : g1 * GROUP // 16]),
-            )
+        def gather(pair, e0, e1):
+            nc.vector.tensor_copy(picked[:, pair, e0 * C : e1 * C], pairs[pair][:].indirect(listed(e0, e1)))
 
-        round_pair(0)
-        gather(0, 0, 3, 0)
-        round_pair(1)
-        gather(1, 0, 3, 3)
-        round_pair(2)
-        gather(2, 0, 3, 6)
-        round_pair(3)
-        round_pair(4)
-
-        woven = []
-        for g in range(GROUPS):
-            woven.append(shared.tile([P, 2, PASSES, C, 2], U32, name="woven%d" % g, offset=g * PASSES * GROUP * 8, align_bytes=64))
+        def gather_woven(pair):
+            a, u = divmod(pair, 2)
+            nc.vector.tensor_copy(woven[0, a][:, :, u], pairs[pair][:].indirect(listed(0, 1)))
 
         def weave(g, a, on_scalar):
-            two = picked[:, 6 * a + g : 6 * a + 6 : 3, :]
+            e0, e1 = GROUPS[g]
+            two = picked[:, 2 * a : 2 * a + 2, e0 * C : e1 * C]
             if on_scalar:
                 nc.scalar.copy(
-                    out=woven[g][:, :, a].rearrange("p e (c i) u -> p e c u i", i=4),
-                    in_=two.rearrange("p u (e c i) -> p e c u i", e=2, i=4),
+                    out=woven[g, a].rearrange("p (c i) u -> p c u i", i=4),
+                    in_=two.rearrange("p u (c i) -> p c u i", i=4),
                 )
             else:
-                nc.gpsimd.tensor_copy(out=woven[g][:, :, a], in_=two.rearrange("p u (e s) -> p e s u", e=2))
+                nc.gpsimd.tensor_copy(out=woven[g, a], in_=two.rearrange("p u s -> p s u"))
 
-        def quantise(e0, e1):
-            g, i = divmod(e0, 2)
-            cols = slice(i * PASSES * C, (i + e1 - e0) * PASSES * C)
-            nc.vector.quantize_mx(
-                out=codes[:, g, cols].bitcast(FP8X4),
-                scales=plane[:, g, cols],
-                in_=woven[g][:, i : i + e1 - e0].rearrange("p e a s u -> p (e a s u)").bitcast(BF16),
-            )
+        def quantise(key):
+            if key == 1:
+                values = woven[key].rearrange("p a s u -> p (a s u)")
+            else:
+                values = woven[key].rearrange("p s u -> p (s u)")
+            nc.vector.quantize_mx(out=codes[key].bitcast(FP8X4), scales=planes[key], in_=values.bitcast(BF16))
 
-        for g in range(GROUPS):
-            gather(3, g, g + 1, 9 + g)
-        for g in range(GROUPS):
-            weave(g, 0, g < GROUPS - 1)
-        for g in range(GROUPS):
-            weave(g, 1, g > 0)
-        for e0, e1 in ((0, 1), (1, 2), (2, 4), (4, 6)):
-            quantise(e0, e1)
+        def products(acc, e, m):
+            g = [h for h in range(len(GROUPS)) if GROUPS[h][0] <= e][-1]
+            i = e - GROUPS[g][0]
+            for a in range(PASSES):
+                if a == 0:
+                    w_codes = w8[g][:, i, 4 * P * m : 4 * P * (m + 1)].bitcast(FP8X4)
+                    w_scale = w8_planes[e // 4][w8_row(e) :, P * m : P * (m + 1)]
+                else:
+                    w_codes = w4[g][:, i, 2 * P * m : 2 * P * (m + 1)].bitcast(FP4X4)
+                    w_scale = w4_plane[:, e, P * m : P * (m + 1)]
+                nc.tensor.matmul_mx(
+                    out=acc,
+                    lhsT=w_codes,
+                    lhsT_scale=w_scale,
+                    rhs=codes[g, a][:, i * C : (i + 1) * C].bitcast(FP8X4),
+                    rhs_scale=planes[g, a][:, i * C : (i + 1) * C],
+                    start=(a == 0),
+                    stop=(a == PASSES - 1),
+                )
 
-        results = []
-        for m in range(N_BLOCKS):
-            results.append(keep.tile([P, S], F32, name="result%d" % m))
+        results = keep.tile([P, N_BLOCKS, S], F32, name="results")
+        rows = {1: 0, 2: 1, 0: 2}
 
-        def multiply(run, m):
-            e0, e1 = run
-            acc = psum.tile([P, (e1 - e0) * C], F32, name="acc%d_%d" % (e0, m))
-            for e in range(e0, e1):
-                g, i = divmod(e, 2)
-                for a in range(PASSES):
-                    cols = slice((i * PASSES + a) * C, (i * PASSES + a + 1) * C)
-                    if a == 0:
-                        w_codes = w8[:, e, 4 * P * m : 4 * P * (m + 1)].bitcast(FP8X4)
-                        w_scale = w8_plane[W8_ROW:, e, P * m : P * (m + 1)]
-                    else:
-                        w_codes = w4[:, e, 2 * P * m : 2 * P * (m + 1)].bitcast(FP4X4)
-                        w_scale = w4_plane[:, e, P * m : P * (m + 1)]
-                    nc.tensor.matmul_mx(
-                        out=acc[:, (e - e0) * C : (e - e0 + 1) * C],
-                        lhsT=w_codes,
-                        lhsT_scale=w_scale,
-                        rhs=codes[:, g, cols].bitcast(FP8X4),
-                        rhs_scale=plane[:, g, cols],
-                        start=(a == 0),
-                        stop=(a == PASSES - 1),
-                    )
-            nc.scalar.copy(out=results[m][:, e0 * C : e1 * C], in_=acc[:])
+        def multiply(e0, e1, blocks):
+            acc = psum.tile([P, len(blocks), (e1 - e0) * C], F32, name="acc%d_%d" % (e0, blocks[0]))
+            for b, m in enumerate(blocks):
+                for e in range(e0, e1):
+                    products(acc[:, b, (e - e0) * C : (e - e0 + 1) * C], e, m)
+            return acc
 
-        steps = [((0, 1), 0), ((0, 2), 1), ((1, 2), 0), ((0, 2), 2)] + [(RUNS[1], m) for m in range(N_BLOCKS)]
-        for run, m in steps:
-            multiply(run, m)
-
-        for (e0, e1), m in steps:
+        def empty(acc, e0, e1, blocks, weights):
+            n = (e1 - e0) * C
+            r = rows[blocks[0]]
             nc.vector.tensor_tensor(
-                windows[m][:].indirect(offsets[:, e0 * C // 16 : e1 * C // 16]),
-                results[m][:, e0 * C : e1 * C],
-                gates[:, e0 * C : e1 * C],
+                results[:, r : r + len(blocks), e0 * C : e1 * C],
+                acc[:],
+                weights.unsqueeze(1).to_broadcast([P, len(blocks), n]),
                 MULT,
             )
-        for m in range(N_BLOCKS):
+
+        def scatter(e0, e1, m, on_scalar):
+            values = results[:, rows[m], e0 * C : e1 * C]
+            if on_scalar:
+                nc.scalar.activation(windows[m][:].indirect(listed(e0, e1)), values, COPY)
+            else:
+                nc.vector.tensor_copy(windows[m][:].indirect(listed(e0, e1)), values)
+
+        for pair in range(3):
+            round_pair(pair)
+            if pair == 2:
+                round_pair(3)
+            gather(pair, 1, E)
+            gather_woven(pair)
+            if pair == 1:
+                quantise((0, 0))
+        weave(1, 0, False)
+        round_pair(4)
+        weave(2, 0, True)
+        gate_again = picked[:, 3, 5 * C : 6 * C].bitcast(F32)
+        nc.scalar.copy(out=gate_again, in_=gate_tiles[0])
+        gather_woven(3)
+        gather(3, 1, 3)
+        quantise((0, 1))
+        weave(1, 1, False)
+        gather(3, 3, 4)
+        first, second = multiply(0, 1, [1]), multiply(0, 1, [2, 0])
+        empty(first, 0, 1, [1], gate_tiles[0])
+        empty(second, 0, 1, [2, 0], gate_again)
+        for m in (1, 2, 0):
+            scatter(0, 1, m, True)
+        quantise(1)
+        gather(3, 4, 6)
+        quantise((2, 0))
+        weave(2, 1, False)
+        for m in (1, 2, 0):
+            empty(multiply(1, 3, [m]), 1, 3, [m], gate_tiles[1])
+            if m > 0:
+                scatter(1, 3, m, True)
+        quantise((2, 1))
+        scatter(1, 3, 0, False)
+        for m in (1, 0, 2):
+            empty(multiply(3, 6, [m]), 3, 6, [m], gate_tiles[3])
+        for m in (1, 0, 2):
+            scatter(3, 6, m, m > 0)
+        for m in (1, 0, 2):
             nc.sync.dma_start(out=out[m * P : (m + 1) * P, :], in_=windows[m][:])

@@ -21,7 +21,7 @@ S = E * C
 N_BLOCKS = N // P
 PASSES = K // K_PASS
 PAIRS = 4
-GROUPS = [(0, 1), (1, 3), (3, 6)]
+RUNS = [(0, 2), (2, 4), (4, 6)]
 
 FLOPS = 2 * S * K * N
 BYTES = 4 * K * T + E * N * (4 * P + 2 * P + 2 * 16) + 4 * S + 2 * S + 4 * N * T
@@ -43,10 +43,10 @@ def tile_moe_pln_lin_none_kernel(tc, xT, w8_words, w8_scales, w4_words, w4_scale
 
         raws = []
         for i, (pair, t0, width, unused) in enumerate(LOADS):
-            if i < 3:
+            if i < 4:
                 raws.append(keep.tile([P, 2, width], F32, name="raw%d" % i))
             else:
-                raws.append(shared.tile([P, 2, width], F32, name="raw%d" % i, offset=1024 + (i - 3) * 7168, align_bytes=64))
+                raws.append(shared.tile([P, 2, width], F32, name="raw%d" % i, offset=0, align_bytes=64))
 
         def load_x(i):
             pair, t0, width, unused = LOADS[i]
@@ -55,12 +55,10 @@ def tile_moe_pln_lin_none_kernel(tc, xT, w8_words, w8_scales, w4_words, w4_scale
             nc.sync.dma_start(out=raws[i][:], in_=rows[:, 2 * u : 2 * u + 2, :])
 
         w8, w4, gates = [], [], []
-        for g, (e0, e1) in enumerate(GROUPS):
-            w8.append(keep.tile([P, e1 - e0, 4 * N], U8, name="w8_%d" % g, align_bytes=64))
-            w4.append(keep.tile([P, e1 - e0, 2 * N], U8, name="w4_%d" % g, align_bytes=64))
-        gate_tiles = {}
-        for e0, e1, m, place in [(0, 1, 0, 18176), (1, 3, 0, 24576), (3, 6, 0, 28672)]:
-            gate_tiles[e0] = shared.tile([P, (e1 - e0) * C], F32, name="gate%d" % e0, offset=place, align_bytes=64)[:]
+        for g in range(len(RUNS)):
+            w8.append(keep.tile([P, 2, 4 * N], U8, name="w8_%d" % g, align_bytes=64))
+            w4.append(keep.tile([P, 2, 2 * N], U8, name="w4_%d" % g, align_bytes=64))
+        gates = keep.tile([P, S], F32, name="gates")
         w8_planes = [keep.tile([P, N], U8, name="w8_plane%d" % h, align_bytes=64) for h in range(2)]
         w4_plane = keep.tile([P, E, N], U8, name="w4_plane", align_bytes=64)
 
@@ -83,12 +81,12 @@ def tile_moe_pln_lin_none_kernel(tc, xT, w8_words, w8_scales, w4_words, w4_scale
                 )
 
         def load_weights(g):
-            es = slice(GROUPS[g][0], GROUPS[g][1])
+            es = slice(RUNS[g][0], RUNS[g][1])
             nc.sync.dma_start(out=w8[g][:].bitcast(I32), in_=w8_words[es, 0].rearrange("e p n r -> p e (n r)").bitcast(I32))
             nc.sync.dma_start(out=w4[g][:].bitcast(I32), in_=w4_words[es, 0].rearrange("e p b -> p e b").bitcast(I32))
 
         def load_gate(e0, e1):
-            nc.sync.dma_start(out=gate_tiles[e0], in_=gate[0:P, e0 * C : e1 * C])
+            nc.sync.dma_start(out=gates[:, e0 * C : e1 * C], in_=gate[0:P, e0 * C : e1 * C])
 
         load_x(0)
         nc.sync.dma_start(offsets[:], offs)
@@ -97,13 +95,12 @@ def tile_moe_pln_lin_none_kernel(tc, xT, w8_words, w8_scales, w4_words, w4_scale
         load_x(2)
         load_x(3)
         load_x(4)
-        load_gate(0, 1)
         load_weights(0)
         load_w4_scales()
+        load_gate(0, 2)
         load_weights(1)
-        load_gate(1, 3)
+        load_gate(2, 6)
         load_weights(2)
-        load_gate(3, 6)
         load_w8_scales(1)
 
         windows = []
@@ -115,29 +112,28 @@ def tile_moe_pln_lin_none_kernel(tc, xT, w8_words, w8_scales, w4_words, w4_scale
                 nc.scalar.copy(out=windows[m][:], in_=windows[0][:])
 
         pairs = [keep.tile([P, T], U32, name="pair%d" % u, align_bytes=64) for u in range(PAIRS)]
-        picked = keep.tile([P, PAIRS, S], U32, name="picked", align_bytes=64)
-        woven, codes, planes = {}, {}, {}
-        for g, (e0, e1) in enumerate(GROUPS):
+        picked = keep.tile([P, PAIRS, 4 * C], U32, name="picked", align_bytes=64)
+
+        pieces = [(0, 0, 2), (0, 2, 6), (1, 0, 1), (1, 1, 2), (1, 2, 4), (1, 4, 6)]
+        woven_at = {(0, 2, 6): 0, (1, 2, 4): 4096, (1, 4, 6): 4096}
+        codes_at = {(1, 1, 2): 8192 + 1024 - 256, (1, 2, 4): 8192, (0, 2, 6): 8192 + 1024}
+        woven, codes, planes, piece_of = {}, {}, {}, {}
+        for piece in pieces:
+            a, e0, e1 = piece
             n = (e1 - e0) * C
-            if g == 0:
-                woven[g, 0] = keep.tile([P, n, 2], U32, name="woven00", align_bytes=64)[:]
-                woven[g, 1] = picked[:, 3, 3 * C : 5 * C].rearrange("p (s u) -> p s u", u=2)
-            elif g == 1:
-                both = shared.tile([P, PASSES, n, 2], U32, name="woven%d" % g, offset=2048, align_bytes=64)
-                woven[g] = both[:]
-                woven[g, 0], woven[g, 1] = both[:, 0], both[:, 1]
+            if piece == (1, 0, 1):
+                woven[piece] = picked[:, 3, 0 : 2 * C].rearrange("p (s u) -> p s u", u=2)
+            elif piece in woven_at:
+                woven[piece] = shared.tile([P, n, 2], U32, name="woven%d%d" % (a, e0), offset=woven_at[piece], align_bytes=64)[:]
             else:
-                woven[g, 0] = shared.tile([P, n, 2], U32, name="woven20", offset=8192, align_bytes=64)[:]
-                woven[g, 1] = shared.tile([P, n, 2], U32, name="woven21", offset=13312, align_bytes=64)[:]
-            if g == 1:
-                both = shared.tile([P, PASSES * n], U32, name="codes1", offset=16384, align_bytes=64)
-                codes[g], codes[g, 0], codes[g, 1] = both[:], both[:, 0:n], both[:, n : 2 * n]
+                woven[piece] = keep.tile([P, n, 2], U32, name="woven%d%d" % (a, e0), align_bytes=64)[:]
+            if piece in codes_at:
+                codes[piece] = shared.tile([P, n], U32, name="codes%d%d" % (a, e0), offset=codes_at[piece], align_bytes=64)[:]
             else:
-                for a in range(PASSES):
-                    place = 12288 + 512 * a if g == 0 else (18432, 20480)[a]
-                    codes[g, a] = shared.tile([P, n], U32, name="codes%d%d" % (g, a), offset=place, align_bytes=64)[:]
-            both = keep.tile([P, PASSES * n], U8, name="plane%d" % g, align_bytes=64)
-            planes[g], planes[g, 0], planes[g, 1] = both[:], both[:, 0:n], both[:, n : 2 * n]
+                codes[piece] = keep.tile([P, n], U32, name="codes%d%d" % (a, e0), align_bytes=64)[:]
+            planes[piece] = keep.tile([P, n], U8, name="plane%d%d" % (a, e0), align_bytes=64)[:]
+            for e in range(e0, e1):
+                piece_of[a, e] = piece
 
         def round_pair(i):
             pair, t0, width, share = LOADS[i]
@@ -156,67 +152,63 @@ def tile_moe_pln_lin_none_kernel(tc, xT, w8_words, w8_scales, w4_words, w4_scale
                 nc.gpsimd.tensor_copy(out=halves[:, rest, :], in_=raws[i][:, :, rest].rearrange("p e t -> p t e"))
 
         def gather(pair, e0, e1):
-            nc.vector.tensor_copy(picked[:, pair, e0 * C : e1 * C], pairs[pair][:].indirect(listed(e0, e1)))
+            nc.vector.tensor_copy(picked[:, pair, (e0 - 2) * C : (e1 - 2) * C], pairs[pair][:].indirect(listed(e0, e1)))
 
-        def gather_woven(pair):
+        def gather_woven(pair, e0, e1):
             a, u = divmod(pair, 2)
-            nc.vector.tensor_copy(woven[0, a][:, :, u], pairs[pair][:].indirect(listed(0, 1)))
+            nc.vector.tensor_copy(woven[a, e0, e1][:, :, u], pairs[pair][:].indirect(listed(e0, e1)))
 
-        def weave(g, a, on_scalar):
-            e0, e1 = GROUPS[g]
-            two = picked[:, 2 * a : 2 * a + 2, e0 * C : e1 * C]
+        def weave(a, e0, e1, on_scalar):
+            piece = piece_of[a, e0]
+            two = picked[:, 2 * a : 2 * a + 2, (e0 - 2) * C : (e1 - 2) * C]
+            both = woven[piece][:, (e0 - piece[1]) * C : (e1 - piece[1]) * C, :]
             if on_scalar:
-                nc.scalar.copy(
-                    out=woven[g, a].rearrange("p (c i) u -> p c u i", i=4),
-                    in_=two.rearrange("p u (c i) -> p c u i", i=4),
-                )
+                nc.scalar.copy(out=both.rearrange("p (c i) u -> p c u i", i=4), in_=two.rearrange("p u (c i) -> p c u i", i=4))
             else:
-                nc.gpsimd.tensor_copy(out=woven[g, a], in_=two.rearrange("p u s -> p s u"))
+                nc.gpsimd.tensor_copy(out=both, in_=two.rearrange("p u s -> p s u"))
 
-        def quantise(key):
-            if key == 1:
-                values = woven[key].rearrange("p a s u -> p (a s u)")
+        def quantise(piece):
+            values = woven[piece].rearrange("p s u -> p (s u)").bitcast(BF16)
+            nc.vector.quantize_mx(out=codes[piece].bitcast(FP8X4), scales=planes[piece], in_=values)
+
+        def product(acc, e, m, a):
+            g, i = divmod(e, 2)
+            piece = piece_of[a, e]
+            cols = slice((e - piece[1]) * C, (e - piece[1] + 1) * C)
+            if a == 0:
+                w_codes = w8[g][:, i, 4 * P * m : 4 * P * (m + 1)].bitcast(FP8X4)
+                w_scale = w8_planes[e // 4][w8_row(e) :, P * m : P * (m + 1)]
             else:
-                values = woven[key].rearrange("p s u -> p (s u)")
-            nc.vector.quantize_mx(out=codes[key].bitcast(FP8X4), scales=planes[key], in_=values.bitcast(BF16))
-
-        def products(acc, e, m):
-            g = [h for h in range(len(GROUPS)) if GROUPS[h][0] <= e][-1]
-            i = e - GROUPS[g][0]
-            for a in range(PASSES):
-                if a == 0:
-                    w_codes = w8[g][:, i, 4 * P * m : 4 * P * (m + 1)].bitcast(FP8X4)
-                    w_scale = w8_planes[e // 4][w8_row(e) :, P * m : P * (m + 1)]
-                else:
-                    w_codes = w4[g][:, i, 2 * P * m : 2 * P * (m + 1)].bitcast(FP4X4)
-                    w_scale = w4_plane[:, e, P * m : P * (m + 1)]
-                nc.tensor.matmul_mx(
-                    out=acc,
-                    lhsT=w_codes,
-                    lhsT_scale=w_scale,
-                    rhs=codes[g, a][:, i * C : (i + 1) * C].bitcast(FP8X4),
-                    rhs_scale=planes[g, a][:, i * C : (i + 1) * C],
-                    start=(a == 0),
-                    stop=(a == PASSES - 1),
-                )
+                w_codes = w4[g][:, i, 2 * P * m : 2 * P * (m + 1)].bitcast(FP4X4)
+                w_scale = w4_plane[:, e, P * m : P * (m + 1)]
+            nc.tensor.matmul_mx(
+                out=acc,
+                lhsT=w_codes,
+                lhsT_scale=w_scale,
+                rhs=codes[piece][:, cols].bitcast(FP8X4),
+                rhs_scale=planes[piece][:, cols],
+                start=(a == 0),
+                stop=(a == PASSES - 1),
+            )
 
         results = keep.tile([P, N_BLOCKS, S], F32, name="results")
         rows = {1: 0, 2: 1, 0: 2}
 
-        def multiply(e0, e1, blocks):
-            acc = psum.tile([P, len(blocks), (e1 - e0) * C], F32, name="acc%d_%d" % (e0, blocks[0]))
+        def multiply(e0, e1, blocks, bank):
+            acc = psum.tile([P, len(blocks), (e1 - e0) * C], F32, name="acc%d_%d" % (e0, blocks[0]), tag="bank%d" % bank)
             for b, m in enumerate(blocks):
                 for e in range(e0, e1):
-                    products(acc[:, b, (e - e0) * C : (e - e0 + 1) * C], e, m)
+                    for a in range(PASSES):
+                        product(acc[:, b, (e - e0) * C : (e - e0 + 1) * C], e, m, a)
             return acc
 
-        def empty(acc, e0, e1, blocks, weights):
+        def empty(acc, e0, e1, blocks):
             n = (e1 - e0) * C
             r = rows[blocks[0]]
             nc.vector.tensor_tensor(
                 results[:, r : r + len(blocks), e0 * C : e1 * C],
                 acc[:],
-                weights.unsqueeze(1).to_broadcast([P, len(blocks), n]),
+                gates[:, e0 * C : e1 * C].unsqueeze(1).to_broadcast([P, len(blocks), n]),
                 MULT,
             )
 
@@ -227,42 +219,44 @@ def tile_moe_pln_lin_none_kernel(tc, xT, w8_words, w8_scales, w4_words, w4_scale
             else:
                 nc.vector.tensor_copy(windows[m][:].indirect(listed(e0, e1)), values)
 
-        for pair in range(3):
+        for pair in range(2):
             round_pair(pair)
-            if pair == 2:
-                round_pair(3)
-            gather(pair, 1, E)
-            gather_woven(pair)
-            if pair == 1:
-                quantise((0, 0))
-        weave(1, 0, False)
+            gather(pair, 2, E)
+            gather_woven(pair, 0, 2)
+        quantise((0, 0, 2))
+        round_pair(2)
+        round_pair(3)
+        gather_woven(2, 0, 1)
+        gather_woven(2, 1, 2)
+        gather(2, 2, 4)
         round_pair(4)
-        weave(2, 0, True)
-        gate_again = picked[:, 3, 5 * C : 6 * C].bitcast(F32)
-        nc.scalar.copy(out=gate_again, in_=gate_tiles[0])
-        gather_woven(3)
-        gather(3, 1, 3)
-        quantise((0, 1))
-        weave(1, 1, False)
-        gather(3, 3, 4)
-        first, second = multiply(0, 1, [1]), multiply(0, 1, [2, 0])
-        empty(first, 0, 1, [1], gate_tiles[0])
-        empty(second, 0, 1, [2, 0], gate_again)
-        for m in (1, 2, 0):
-            scatter(0, 1, m, True)
-        quantise(1)
-        gather(3, 4, 6)
-        quantise((2, 0))
-        weave(2, 1, False)
-        for m in (1, 2, 0):
-            empty(multiply(1, 3, [m]), 1, 3, [m], gate_tiles[1])
-            if m > 0:
-                scatter(1, 3, m, True)
-        quantise((2, 1))
+        weave(0, 2, 4, True)
+        weave(0, 4, 6, True)
+        gather_woven(3, 0, 1)
+        gather_woven(3, 1, 2)
+        quantise((1, 0, 1))
+        quantise((1, 1, 2))
+        gather(3, 2, 4)
+        weave(1, 2, 4, False)
+        for e0, e1, blocks, bank in [(0, 1, [1], 0), (0, 1, [2, 0], 1), (1, 2, [1, 2, 0], 2)]:
+            empty(multiply(e0, e1, blocks, bank), e0, e1, blocks)
+        for e, m in [(0, 1), (0, 2), (0, 0), (1, 1), (1, 2)]:
+            scatter(e, e + 1, m, True)
+        quantise((1, 2, 4))
+        quantise((0, 2, 6))
+        gather_woven(2, 4, 6)
+        gather_woven(3, 4, 6)
+        accs = [multiply(2, 4, [m], 3 + m) for m in (1, 0, 2)]
+        empty(accs[0], 2, 4, [1])
+        quantise((1, 4, 6))
+        empty(accs[1], 2, 4, [0])
+        empty(accs[2], 2, 4, [2])
+        scatter(2, 4, 1, True)
+        scatter(2, 3, 2, True)
         scatter(1, 3, 0, False)
+        for m, bank in ((1, 6), (0, 7), (2, 0)):
+            empty(multiply(4, 6, [m], bank), 4, 6, [m])
         for m in (1, 0, 2):
-            empty(multiply(3, 6, [m]), 3, 6, [m], gate_tiles[3])
-        for m in (1, 0, 2):
-            scatter(3, 6, m, m > 0)
+            scatter(4 if m == 1 else 3, 6, m, m > 0)
         for m in (1, 0, 2):
             nc.sync.dma_start(out=out[m * P : (m + 1) * P, :], in_=windows[m][:])

@@ -21,7 +21,9 @@ S = E * C
 N_BLOCKS = N // P
 PASSES = K // K_PASS
 PAIRS = 4
-RUNS = [(0, 2), (2, 4), (4, 6)]
+RUNS = [(0, 1), (1, 2), (2, 4), (4, 6)]
+
+CUT = 320
 
 FLOPS = 2 * S * K * N
 BYTES = 4 * K * T + E * N * (4 * P + 2 * P + 2 * 16) + 4 * S + 2 * S + 4 * N * T
@@ -38,15 +40,15 @@ def tile_moe_pln_lin_none_kernel(tc, xT, w8_words, w8_scales, w4_words, w4_scale
 
         offsets = keep.tile([P, S // 16], U16, name="offsets")
 
-        def listed(e0, e1):
-            return offsets[:, e0 * C // 16 : e1 * C // 16]
+        def listed(s0, s1):
+            return offsets[:, s0 // 16 : s1 // 16]
 
         raws = []
         for i, (pair, t0, width, unused) in enumerate(LOADS):
             if i < 4:
                 raws.append(keep.tile([P, 2, width], F32, name="raw%d" % i))
             else:
-                raws.append(shared.tile([P, 2, width], F32, name="raw%d" % i, offset=0, align_bytes=64))
+                raws.append(shared.tile([P, 2, width], F32, name="raw%d" % i, offset=1024, align_bytes=64))
 
         def load_x(i):
             pair, t0, width, unused = LOADS[i]
@@ -55,10 +57,12 @@ def tile_moe_pln_lin_none_kernel(tc, xT, w8_words, w8_scales, w4_words, w4_scale
             nc.sync.dma_start(out=raws[i][:], in_=rows[:, 2 * u : 2 * u + 2, :])
 
         w8, w4, gates = [], [], []
-        for g in range(len(RUNS)):
-            w8.append(keep.tile([P, 2, 4 * N], U8, name="w8_%d" % g, align_bytes=64))
-            w4.append(keep.tile([P, 2, 2 * N], U8, name="w4_%d" % g, align_bytes=64))
-        gates = keep.tile([P, S], F32, name="gates")
+        for g, (e0, e1) in enumerate(RUNS):
+            w8.append(keep.tile([P, e1 - e0, 4 * N], U8, name="w8_%d" % g, align_bytes=64))
+            w4.append(keep.tile([P, e1 - e0, 2 * N], U8, name="w4_%d" % g, align_bytes=64))
+        picked = keep.tile([P, PAIRS, 5 * C], U32, name="picked", align_bytes=64)
+        gates = keep.tile([P, 4 * C], F32, name="gates")
+        first_gates = picked[:, 2:4, 4 * C : 5 * C].bitcast(F32)
         w8_planes = [keep.tile([P, N], U8, name="w8_plane%d" % h, align_bytes=64) for h in range(2)]
         w4_plane = keep.tile([P, E, N], U8, name="w4_plane", align_bytes=64)
 
@@ -85,8 +89,8 @@ def tile_moe_pln_lin_none_kernel(tc, xT, w8_words, w8_scales, w4_words, w4_scale
             nc.sync.dma_start(out=w8[g][:].bitcast(I32), in_=w8_words[es, 0].rearrange("e p n r -> p e (n r)").bitcast(I32))
             nc.sync.dma_start(out=w4[g][:].bitcast(I32), in_=w4_words[es, 0].rearrange("e p b -> p e b").bitcast(I32))
 
-        def load_gate(e0, e1):
-            nc.sync.dma_start(out=gates[:, e0 * C : e1 * C], in_=gate[0:P, e0 * C : e1 * C])
+        def gate_of(e0, e1):
+            return first_gates[:, e0, :] if e0 < 2 else gates[:, (e0 - 2) * C : (e1 - 2) * C]
 
         load_x(0)
         nc.sync.dma_start(offsets[:], offs)
@@ -97,10 +101,11 @@ def tile_moe_pln_lin_none_kernel(tc, xT, w8_words, w8_scales, w4_words, w4_scale
         load_x(4)
         load_weights(0)
         load_w4_scales()
-        load_gate(0, 2)
+        nc.sync.dma_start(out=first_gates, in_=gate[0:P, 0 : 2 * C].rearrange("p (e c) -> p e c", e=2))
         load_weights(1)
-        load_gate(2, 6)
         load_weights(2)
+        nc.sync.dma_start(out=gates[:], in_=gate[0:P, 2 * C : S])
+        load_weights(3)
         load_w8_scales(1)
 
         windows = []
@@ -112,17 +117,26 @@ def tile_moe_pln_lin_none_kernel(tc, xT, w8_words, w8_scales, w4_words, w4_scale
                 nc.scalar.copy(out=windows[m][:], in_=windows[0][:])
 
         pairs = [keep.tile([P, T], U32, name="pair%d" % u, align_bytes=64) for u in range(PAIRS)]
-        picked = keep.tile([P, PAIRS, 4 * C], U32, name="picked", align_bytes=64)
 
-        pieces = [(0, 0, 2), (0, 2, 6), (1, 0, 1), (1, 1, 2), (1, 2, 4), (1, 4, 6)]
-        woven_at = {(0, 2, 6): 0, (1, 2, 4): 4096, (1, 4, 6): 4096}
-        codes_at = {(1, 1, 2): 8192 + 1024 - 256, (1, 2, 4): 8192, (0, 2, 6): 8192 + 1024}
+        pieces = [(0, 0, 1), (1, 0, 1), (0, 1, 2), (1, 1, 2), (0, 2, 4), (1, 2, 4), (0, 4, 6), (1, 4, 6)]
+        woven_at = {(0, 2, 4): 2048, (0, 4, 6): 4096, (1, 2, 4): 0, (1, 4, 6): 4096}
+        codes_at = {(1, 0, 1): 8192, (0, 2, 4): 9216, (1, 2, 4): 7680, (0, 4, 6): 2048}
         woven, codes, planes, piece_of = {}, {}, {}, {}
+        second = shared.tile([P, PASSES * C, 2], U32, name="woven_second", offset=0, align_bytes=64)
+        second_codes = shared.tile([P, PASSES * C], U32, name="codes_second", offset=8448, align_bytes=64)
+        second_plane = keep.tile([P, PASSES * C], U8, name="plane_second", align_bytes=64)
+        woven[1], codes[1], planes[1] = second[:], second_codes[:], second_plane[:]
         for piece in pieces:
             a, e0, e1 = piece
             n = (e1 - e0) * C
+            for e in range(e0, e1):
+                piece_of[a, e] = piece
+            if e0 == 1:
+                cols = slice(a * C, (a + 1) * C)
+                woven[piece], codes[piece], planes[piece] = second[:, cols, :], second_codes[:, cols], second_plane[:, cols]
+                continue
             if piece == (1, 0, 1):
-                woven[piece] = picked[:, 3, 0 : 2 * C].rearrange("p (s u) -> p s u", u=2)
+                woven[piece] = picked[:, 3, C : 3 * C].rearrange("p (s u) -> p s u", u=2)
             elif piece in woven_at:
                 woven[piece] = shared.tile([P, n, 2], U32, name="woven%d%d" % (a, e0), offset=woven_at[piece], align_bytes=64)[:]
             else:
@@ -132,8 +146,6 @@ def tile_moe_pln_lin_none_kernel(tc, xT, w8_words, w8_scales, w4_words, w4_scale
             else:
                 codes[piece] = keep.tile([P, n], U32, name="codes%d%d" % (a, e0), align_bytes=64)[:]
             planes[piece] = keep.tile([P, n], U8, name="plane%d%d" % (a, e0), align_bytes=64)[:]
-            for e in range(e0, e1):
-                piece_of[a, e] = piece
 
         def round_pair(i):
             pair, t0, width, share = LOADS[i]
@@ -152,15 +164,15 @@ def tile_moe_pln_lin_none_kernel(tc, xT, w8_words, w8_scales, w4_words, w4_scale
                 nc.gpsimd.tensor_copy(out=halves[:, rest, :], in_=raws[i][:, :, rest].rearrange("p e t -> p t e"))
 
         def gather(pair, e0, e1):
-            nc.vector.tensor_copy(picked[:, pair, (e0 - 2) * C : (e1 - 2) * C], pairs[pair][:].indirect(listed(e0, e1)))
+            nc.vector.tensor_copy(picked[:, pair, (e0 - 1) * C : (e1 - 1) * C], pairs[pair][:].indirect(listed(e0 * C, e1 * C)))
 
         def gather_woven(pair, e0, e1):
             a, u = divmod(pair, 2)
-            nc.vector.tensor_copy(woven[a, e0, e1][:, :, u], pairs[pair][:].indirect(listed(e0, e1)))
+            nc.vector.tensor_copy(woven[a, e0, e1][:, :, u], pairs[pair][:].indirect(listed(e0 * C, e1 * C)))
 
         def weave(a, e0, e1, on_scalar):
             piece = piece_of[a, e0]
-            two = picked[:, 2 * a : 2 * a + 2, (e0 - 2) * C : (e1 - 2) * C]
+            two = picked[:, 2 * a : 2 * a + 2, (e0 - 1) * C : (e1 - 1) * C]
             both = woven[piece][:, (e0 - piece[1]) * C : (e1 - piece[1]) * C, :]
             if on_scalar:
                 nc.scalar.copy(out=both.rearrange("p (c i) u -> p c u i", i=4), in_=two.rearrange("p u (c i) -> p c u i", i=4))
@@ -172,7 +184,8 @@ def tile_moe_pln_lin_none_kernel(tc, xT, w8_words, w8_scales, w4_words, w4_scale
             nc.vector.quantize_mx(out=codes[piece].bitcast(FP8X4), scales=planes[piece], in_=values)
 
         def product(acc, e, m, a):
-            g, i = divmod(e, 2)
+            g = [h for h in range(len(RUNS)) if RUNS[h][0] <= e][-1]
+            i = e - RUNS[g][0]
             piece = piece_of[a, e]
             cols = slice((e - piece[1]) * C, (e - piece[1] + 1) * C)
             if a == 0:
@@ -208,55 +221,57 @@ def tile_moe_pln_lin_none_kernel(tc, xT, w8_words, w8_scales, w4_words, w4_scale
             nc.vector.tensor_tensor(
                 results[:, r : r + len(blocks), e0 * C : e1 * C],
                 acc[:],
-                gates[:, e0 * C : e1 * C].unsqueeze(1).to_broadcast([P, len(blocks), n]),
+                gate_of(e0, e1).unsqueeze(1).to_broadcast([P, len(blocks), n]),
                 MULT,
             )
 
-        def scatter(e0, e1, m, on_scalar):
-            values = results[:, rows[m], e0 * C : e1 * C]
+        def scatter(s0, s1, m, on_scalar):
+            values = results[:, rows[m], s0:s1]
             if on_scalar:
-                nc.scalar.activation(windows[m][:].indirect(listed(e0, e1)), values, COPY)
+                nc.scalar.activation(windows[m][:].indirect(listed(s0, s1)), values, COPY)
             else:
-                nc.vector.tensor_copy(windows[m][:].indirect(listed(e0, e1)), values)
+                nc.vector.tensor_copy(windows[m][:].indirect(listed(s0, s1)), values)
 
         for pair in range(2):
             round_pair(pair)
-            gather(pair, 2, E)
-            gather_woven(pair, 0, 2)
-        quantise((0, 0, 2))
+            gather(pair, 1, E)
+            gather_woven(pair, 0, 1)
+        quantise((0, 0, 1))
         round_pair(2)
         round_pair(3)
+        gather(2, 1, 4)
         gather_woven(2, 0, 1)
-        gather_woven(2, 1, 2)
-        gather(2, 2, 4)
         round_pair(4)
+        weave(0, 1, 2, True)
         weave(0, 2, 4, True)
-        weave(0, 4, 6, True)
+        weave(0, 4, 6, False)
         gather_woven(3, 0, 1)
-        gather_woven(3, 1, 2)
+        gather(3, 1, 2)
+        weave(1, 1, 2, True)
         quantise((1, 0, 1))
-        quantise((1, 1, 2))
         gather(3, 2, 4)
+        for blocks, bank in [([1], 0), ([2, 0], 1)]:
+            empty(multiply(0, 1, blocks, bank), 0, 1, blocks)
+        quantise(1)
         weave(1, 2, 4, False)
-        for e0, e1, blocks, bank in [(0, 1, [1], 0), (0, 1, [2, 0], 1), (1, 2, [1, 2, 0], 2)]:
-            empty(multiply(e0, e1, blocks, bank), e0, e1, blocks)
+        gather(2, 4, 6)
+        empty(multiply(1, 2, [1, 2, 0], 2), 1, 2, [1, 2, 0])
         for e, m in [(0, 1), (0, 2), (0, 0), (1, 1), (1, 2)]:
-            scatter(e, e + 1, m, True)
+            scatter(e * C, (e + 1) * C, m, True)
+        quantise((0, 2, 4))
         quantise((1, 2, 4))
-        quantise((0, 2, 6))
-        gather_woven(2, 4, 6)
-        gather_woven(3, 4, 6)
-        accs = [multiply(2, 4, [m], 3 + m) for m in (1, 0, 2)]
-        empty(accs[0], 2, 4, [1])
+        gather(3, 4, 6)
+        quantise((0, 4, 6))
+        weave(1, 4, 6, False)
+        for m in (1, 0, 2):
+            empty(multiply(2, 4, [m], 3 + m), 2, 4, [m])
         quantise((1, 4, 6))
-        empty(accs[1], 2, 4, [0])
-        empty(accs[2], 2, 4, [2])
-        scatter(2, 4, 1, True)
-        scatter(2, 3, 2, True)
-        scatter(1, 3, 0, False)
+        scatter(2 * C, 4 * C, 1, True)
+        scatter(2 * C, 3 * C, 2, True)
+        scatter(C, CUT, 0, False)
         for m, bank in ((1, 6), (0, 7), (2, 0)):
             empty(multiply(4, 6, [m], bank), 4, 6, [m])
         for m in (1, 0, 2):
-            scatter(4 if m == 1 else 3, 6, m, m > 0)
+            scatter({1: 4 * C, 0: CUT, 2: 3 * C}[m], S, m, m > 0)
         for m in (1, 0, 2):
             nc.sync.dma_start(out=out[m * P : (m + 1) * P, :], in_=windows[m][:])

@@ -77,11 +77,11 @@ def tile_moe_pln_lin_none_kernel(tc, xT, w8_words, w8_scales, w4_words, w4_scale
                     in_=w8_scales[e0:e1, 0, 4 * q : 4 * q + 4, :].bitcast(I32),
                 )
 
-        def load_w4_scales():
+        def load_w4_scales(e0, e1):
             for r in range(4):
                 nc.sync.dma_start(
-                    out=w4_plane[r:P:32, :, :].bitcast(I32),
-                    in_=w4_scales[:, 0, r:16:4, :].rearrange("e q n -> q e n").bitcast(I32),
+                    out=w4_plane[r:P:32, e0:e1, :].bitcast(I32),
+                    in_=w4_scales[e0:e1, 0, r:16:4, :].rearrange("e q n -> q e n").bitcast(I32),
                 )
 
         def load_weights(g):
@@ -97,12 +97,13 @@ def tile_moe_pln_lin_none_kernel(tc, xT, w8_words, w8_scales, w4_words, w4_scale
         load_x(1)
         load_w8_scales(0)
         load_x(2)
+        load_w4_scales(0, 2)
         load_x(3)
         load_x(4)
         load_weights(0)
-        load_w4_scales()
         nc.sync.dma_start(out=first_gates, in_=gate[0:P, 0 : 2 * C].rearrange("p (e c) -> p e c", e=2))
         load_weights(1)
+        load_w4_scales(2, E)
         load_weights(2)
         nc.sync.dma_start(out=gates[:], in_=gate[0:P, 2 * C : S])
         load_weights(3)
@@ -120,7 +121,7 @@ def tile_moe_pln_lin_none_kernel(tc, xT, w8_words, w8_scales, w4_words, w4_scale
 
         pieces = [(0, 0, 1), (1, 0, 1), (0, 1, 2), (1, 1, 2), (0, 2, 4), (1, 2, 4), (0, 4, 6), (1, 4, 6)]
         woven_at = {(0, 2, 4): 2048, (0, 4, 6): 4096, (1, 2, 4): 0, (1, 4, 6): 4096}
-        codes_at = {(1, 0, 1): 8192, (0, 2, 4): 9216, (1, 2, 4): 7680, (0, 4, 6): 2048}
+        codes_at = {(1, 0, 1): 8192, (0, 2, 4): 9216, (1, 2, 4): 7680, (0, 4, 6): 2048, (1, 4, 6): 7680}
         woven, codes, planes, piece_of = {}, {}, {}, {}
         second = shared.tile([P, PASSES * C, 2], U32, name="woven_second", offset=0, align_bytes=64)
         second_codes = shared.tile([P, PASSES * C], U32, name="codes_second", offset=8448, align_bytes=64)

@@ -1,6 +1,7 @@
 from contextlib import ExitStack
 
 import concourse.mybir as mybir
+from concourse.masks import make_identity
 
 F32 = mybir.dt.float32
 BF16 = mybir.dt.bfloat16
@@ -61,8 +62,11 @@ def tile_moe_pln_lin_none_kernel(tc, xT, w8_words, w8_scales, w4_words, w4_scale
             w8.append(keep.tile([P, e1 - e0, 4 * N], U8, name="w8_%d" % g, align_bytes=64))
             w4.append(keep.tile([P, e1 - e0, 2 * N], U8, name="w4_%d" % g, align_bytes=64))
         picked = keep.tile([P, PAIRS, 5 * C], U32, name="picked", align_bytes=64)
-        gates = keep.tile([P, 4 * C], F32, name="gates")
-        first_gates = picked[:, 2:4, 4 * C : 5 * C].bitcast(F32)
+        late = keep.tile([P, 2, 2 * C], U32, name="late", align_bytes=64)
+        gates = keep.tile([P, S], F32, name="gates")
+        gate_columns = keep.tile([P, 2, 3], F32, name="gate_columns")
+        identity = keep.tile([P, P], F32, name="identity")
+        first_gate = late[:].rearrange("p u s -> p (u s)")[:, 3 * C // 2 : 5 * C // 2].bitcast(F32)
         w8_planes = [keep.tile([P, N], U8, name="w8_plane%d" % h, align_bytes=64) for h in range(2)]
         w4_plane = keep.tile([P, E, N], U8, name="w4_plane", align_bytes=64)
 
@@ -90,22 +94,21 @@ def tile_moe_pln_lin_none_kernel(tc, xT, w8_words, w8_scales, w4_words, w4_scale
             nc.sync.dma_start(out=w4[g][:].bitcast(I32), in_=w4_words[es, 0].rearrange("e p b -> p e b").bitcast(I32))
 
         def gate_of(e0, e1):
-            return first_gates[:, e0, :] if e0 < 2 else gates[:, (e0 - 2) * C : (e1 - 2) * C]
+            return first_gate if e0 == 0 else gates[:, e0 * C : e1 * C]
 
+        nc.sync.dma_start(out=gate_columns[:], in_=gate[0, :].rearrange("(h c x) -> c h x", h=2, x=3))
         load_x(0)
         nc.sync.dma_start(offsets[:], offs)
         load_x(1)
         load_w8_scales(0)
         load_x(2)
-        load_w4_scales(0, 2)
         load_x(3)
         load_x(4)
         load_weights(0)
-        nc.sync.dma_start(out=first_gates, in_=gate[0:P, 0 : 2 * C].rearrange("p (e c) -> p e c", e=2))
+        load_w4_scales(0, 2)
         load_weights(1)
         load_w4_scales(2, E)
         load_weights(2)
-        nc.sync.dma_start(out=gates[:], in_=gate[0:P, 2 * C : S])
         load_weights(3)
         load_w8_scales(1)
 
@@ -117,15 +120,24 @@ def tile_moe_pln_lin_none_kernel(tc, xT, w8_words, w8_scales, w4_words, w4_scale
             else:
                 nc.scalar.copy(out=windows[m][:], in_=windows[0][:])
 
+        make_identity(nc, identity[:])
+        for h in range(2):
+            spread = psum.tile([P, 3, P], F32, name="spread%d" % h, tag="bank%d" % (6 + h))
+            for x in range(3):
+                nc.tensor.transpose(spread[:, x, :], gate_columns[:, h, x : x + 1].to_broadcast([P, P]), identity[:])
+            half = gates[:, h * S // 2 : (h + 1) * S // 2]
+            nc.scalar.copy(out=half.rearrange("p (c x) -> p c x", x=3), in_=spread[:].rearrange("p x c -> p c x"))
+        nc.scalar.copy(out=first_gate, in_=gates[:, 0:C])
+
         pairs = [keep.tile([P, T], U32, name="pair%d" % u, align_bytes=64) for u in range(PAIRS)]
 
         pieces = [(0, 0, 1), (1, 0, 1), (0, 1, 2), (1, 1, 2), (0, 2, 4), (1, 2, 4), (0, 4, 6), (1, 4, 6)]
-        woven_at = {(0, 2, 4): 2048, (0, 4, 6): 4096, (1, 2, 4): 0, (1, 4, 6): 4096}
-        codes_at = {(1, 0, 1): 8192, (0, 2, 4): 9216, (1, 2, 4): 7680, (0, 4, 6): 2048, (1, 4, 6): 7680}
+        woven_at = {(0, 2, 4): 2048, (0, 4, 6): 4096, (1, 2, 4): 0, (1, 4, 6): 12288}
+        codes_at = {(1, 0, 1): 8192, (1, 2, 4): 7680, (0, 4, 6): 9216}
         woven, codes, planes, piece_of = {}, {}, {}, {}
         second = shared.tile([P, PASSES * C, 2], U32, name="woven_second", offset=0, align_bytes=64)
         second_codes = shared.tile([P, PASSES * C], U32, name="codes_second", offset=8448, align_bytes=64)
-        second_plane = keep.tile([P, PASSES * C], U8, name="plane_second", align_bytes=64)
+        second_plane = shared.tile([P, PASSES * C], U8, name="plane_second", offset=12288, align_bytes=64)
         woven[1], codes[1], planes[1] = second[:], second_codes[:], second_plane[:]
         for piece in pieces:
             a, e0, e1 = piece
@@ -164,18 +176,28 @@ def tile_moe_pln_lin_none_kernel(tc, xT, w8_words, w8_scales, w4_words, w4_scale
             else:
                 nc.gpsimd.tensor_copy(out=halves[:, rest, :], in_=raws[i][:, :, rest].rearrange("p e t -> p t e"))
 
+        def picked_rows(a, e0, e1):
+            if (a, e0) == (1, 4):
+                return late[:]
+            return picked[:, 2 * a : 2 * a + 2, (e0 - 1) * C : (e1 - 1) * C]
+
         def gather(pair, e0, e1):
-            nc.vector.tensor_copy(picked[:, pair, (e0 - 1) * C : (e1 - 1) * C], pairs[pair][:].indirect(listed(e0 * C, e1 * C)))
+            nc.vector.tensor_copy(picked_rows(pair // 2, e0, e1)[:, pair % 2, :], pairs[pair][:].indirect(listed(e0 * C, e1 * C)))
 
         def gather_woven(pair, e0, e1):
             a, u = divmod(pair, 2)
             nc.vector.tensor_copy(woven[a, e0, e1][:, :, u], pairs[pair][:].indirect(listed(e0 * C, e1 * C)))
 
-        def weave(a, e0, e1, on_scalar):
+        def weave(a, e0, e1, engine):
             piece = piece_of[a, e0]
-            two = picked[:, 2 * a : 2 * a + 2, (e0 - 1) * C : (e1 - 1) * C]
+            two = picked_rows(a, e0, e1)
             both = woven[piece][:, (e0 - piece[1]) * C : (e1 - piece[1]) * C, :]
-            if on_scalar:
+            if engine == "vector":
+                nc.vector.tensor_copy(
+                    out=both.bitcast(I32).rearrange("p (c i) u -> p c u i", i=4),
+                    in_=two.bitcast(I32).rearrange("p u (c i) -> p c u i", i=4),
+                )
+            elif engine == "scalar":
                 nc.scalar.copy(out=both.rearrange("p (c i) u -> p c u i", i=4), in_=two.rearrange("p u (c i) -> p c u i", i=4))
             else:
                 nc.gpsimd.tensor_copy(out=both, in_=two.rearrange("p u s -> p s u"))
@@ -243,30 +265,30 @@ def tile_moe_pln_lin_none_kernel(tc, xT, w8_words, w8_scales, w4_words, w4_scale
         gather(2, 1, 4)
         gather_woven(2, 0, 1)
         round_pair(4)
-        weave(0, 1, 2, True)
-        weave(0, 2, 4, True)
-        weave(0, 4, 6, False)
+        weave(0, 2, 4, "scalar")
+        weave(0, 1, 2, "scalar")
+        weave(0, 4, 6, "gpsimd")
         gather_woven(3, 0, 1)
         gather(3, 1, 2)
-        weave(1, 1, 2, True)
+        weave(1, 1, 2, "scalar")
         quantise((1, 0, 1))
+        quantise((0, 2, 4))
         gather(3, 2, 4)
         for blocks, bank in [([1], 0), ([2, 0], 1)]:
             empty(multiply(0, 1, blocks, bank), 0, 1, blocks)
         quantise(1)
-        weave(1, 2, 4, False)
+        weave(1, 2, 4, "gpsimd")
         gather(2, 4, 6)
+        gather(3, 4, 6)
         empty(multiply(1, 2, [1, 2, 0], 2), 1, 2, [1, 2, 0])
         for e, m in [(0, 1), (0, 2), (0, 0), (1, 1), (1, 2)]:
             scatter(e * C, (e + 1) * C, m, True)
-        quantise((0, 2, 4))
         quantise((1, 2, 4))
-        gather(3, 4, 6)
+        weave(1, 4, 6, "vector")
         quantise((0, 4, 6))
-        weave(1, 4, 6, False)
+        quantise((1, 4, 6))
         for m in (1, 0, 2):
             empty(multiply(2, 4, [m], 3 + m), 2, 4, [m])
-        quantise((1, 4, 6))
         scatter(2 * C, 4 * C, 1, True)
         scatter(2 * C, 3 * C, 2, True)
         scatter(C, CUT, 0, False)

@@ -29,7 +29,7 @@ CUT = 320
 FLOPS = 2 * S * K * N
 BYTES = 4 * K * T + E * N * (4 * P + 2 * P + 2 * 16) + 4 * S + 2 * S + 4 * N * T
 
-LOADS = [(0, 0, 1024, 384), (1, 0, 1024, 512), (2, 0, 1024, 512), (3, 0, 512, 256), (3, 512, 512, 256)]
+LOADS = [(0, 0, 1024, 384), (1, 0, 1024, 512), (2, 0, 1024, 512), (3, 0, 640, 320), (3, 640, 384, 192)]
 
 
 def tile_moe_pln_lin_none_kernel(tc, xT, w8_words, w8_scales, w4_words, w4_scales, gate, offs, out):
@@ -47,15 +47,16 @@ def tile_moe_pln_lin_none_kernel(tc, xT, w8_words, w8_scales, w4_words, w4_scale
         raws = []
         for i, (pair, t0, width, unused) in enumerate(LOADS):
             if i < 4:
-                raws.append(keep.tile([P, 2, width], F32, name="raw%d" % i))
+                raws.append(keep.tile([P, 2, width], F32, name="raw%d" % i)[:])
             else:
-                raws.append(shared.tile([P, 2, width], F32, name="raw%d" % i, offset=1024, align_bytes=64))
+                room = shared.tile([P, 1024], F32, name="raw%d" % i, offset=1024, align_bytes=64)
+                raws.append(room[:, 0 : 2 * width].rearrange("p (e t) -> p e t", e=2))
 
         def load_x(i):
             pair, t0, width, unused = LOADS[i]
             a, u = divmod(pair, 2)
             rows = xT[a * K_PASS : (a + 1) * K_PASS, t0 : t0 + width].rearrange("(p j) t -> p j t", j=PACK)
-            nc.sync.dma_start(out=raws[i][:], in_=rows[:, 2 * u : 2 * u + 2, :])
+            nc.sync.dma_start(out=raws[i], in_=rows[:, 2 * u : 2 * u + 2, :])
 
         w8, w4, gates = [], [], []
         for g, (e0, e1) in enumerate(RUNS):
@@ -96,8 +97,8 @@ def tile_moe_pln_lin_none_kernel(tc, xT, w8_words, w8_scales, w4_words, w4_scale
         def gate_of(e0, e1):
             return first_gate if e0 == 0 else gates[:, e0 * C : e1 * C]
 
-        nc.sync.dma_start(out=gate_columns[:], in_=gate[0, :].rearrange("(h c x) -> c h x", h=2, x=3))
         load_x(0)
+        nc.sync.dma_start(out=gate_columns[:], in_=gate[0, :].rearrange("(h c x) -> c h x", h=2, x=3))
         nc.sync.dma_start(offsets[:], offs)
         load_x(1)
         load_w8_scales(0)

@@ -24,7 +24,7 @@ PASSES = K // K_PASS
 PAIRS = 4
 RUNS = [(0, 1), (1, 2), (2, 4), (4, 6)]
 
-CUT = 320
+CUT = 288
 
 FLOPS = 2 * S * K * N
 BYTES = 4 * K * T + E * N * (4 * P + 2 * P + 2 * 16) + 4 * S + 2 * S + 4 * N * T
@@ -281,19 +281,22 @@ def tile_moe_pln_lin_none_kernel(tc, xT, w8_words, w8_scales, w4_words, w4_scale
         weave(1, 2, 4, "gpsimd")
         gather(2, 4, 6)
         gather(3, 4, 6)
-        empty(multiply(1, 2, [1, 2, 0], 2), 1, 2, [1, 2, 0])
+        accs = [multiply(1, 2, blocks, bank) for blocks, bank in (([1], 2), ([2, 0], 6))]
+        empty(accs[0], 1, 2, [1])
+        quantise((1, 2, 4))
+        empty(accs[1], 1, 2, [2, 0])
         for e, m in [(0, 1), (0, 2), (0, 0), (1, 1), (1, 2)]:
             scatter(e * C, (e + 1) * C, m, True)
-        quantise((1, 2, 4))
         weave(1, 4, 6, "vector")
         quantise((0, 4, 6))
-        quantise((1, 4, 6))
         for m in (1, 0, 2):
             empty(multiply(2, 4, [m], 3 + m), 2, 4, [m])
+            if m == 1:
+                quantise((1, 4, 6))
         scatter(2 * C, 4 * C, 1, True)
         scatter(2 * C, 3 * C, 2, True)
         scatter(C, CUT, 0, False)
-        for m, bank in ((1, 6), (0, 7), (2, 0)):
+        for m, bank in ((1, 7), (0, 0), (2, 1)):
             empty(multiply(4, 6, [m], bank), 4, 6, [m])
         for m in (1, 0, 2):
             scatter({1: 4 * C, 0: CUT, 2: 3 * C}[m], S, m, m > 0)

@@ -23,13 +23,18 @@ N_BLOCKS = N // P
 PASSES = K // K_PASS
 PAIRS = 4
 RUNS = [(0, 1), (1, 2), (2, 4), (4, 6)]
-
-CUT = 288
+WEIGHT_LOADS = [(0, 1), (1, 4), (4, 6)]
+LONG_ROWS = 256
+MX_ALIGN = 64
 
 FLOPS = 2 * S * K * N
 BYTES = 4 * K * T + E * N * (4 * P + 2 * P + 2 * 16) + 4 * S + 2 * S + 4 * N * T
 
-LOADS = [(0, 0, 1024, 384), (1, 0, 1024, 512), (2, 0, 1024, 512), (3, 0, 640, 320), (3, 640, 384, 192)]
+FIRST_SHARE = 384
+MIDDLE_CUT = 448
+MIDDLE_SHARES = (240, 768)
+LAST_CUT = 512
+LAST_SHARE = 656
 
 
 def tile_moe_pln_lin_none_kernel(tc, xT, w8_words, w8_scales, w4_words, w4_scales, gate, offs, out):
@@ -45,31 +50,26 @@ def tile_moe_pln_lin_none_kernel(tc, xT, w8_words, w8_scales, w4_words, w4_scale
             return offsets[:, s0 // 16 : s1 // 16]
 
         raws = []
-        for i, (pair, t0, width, unused) in enumerate(LOADS):
-            if i < 4:
-                raws.append(keep.tile([P, 2, width], F32, name="raw%d" % i)[:])
+        for u in range(PAIRS):
+            if u == 2:
+                raws.append(shared.tile([P, 2 * T], F32, name="raw2", offset=0, align_bytes=LONG_ROWS))
             else:
-                room = shared.tile([P, 1024], F32, name="raw%d" % i, offset=1024, align_bytes=64)
-                raws.append(room[:, 0 : 2 * width].rearrange("p (e t) -> p e t", e=2))
+                raws.append(keep.tile([P, 2 * T], F32, name="raw%d" % u, align_bytes=LONG_ROWS))
 
-        def load_x(i):
-            pair, t0, width, unused = LOADS[i]
+        def load_x(pair, c0, c1):
             a, u = divmod(pair, 2)
-            rows = xT[a * K_PASS : (a + 1) * K_PASS, t0 : t0 + width].rearrange("(p j) t -> p j t", j=PACK)
-            nc.sync.dma_start(out=raws[i], in_=rows[:, 2 * u : 2 * u + 2, :])
+            rows = xT[a * K_PASS : (a + 1) * K_PASS, :].rearrange("(p j) t -> p (j t)", j=PACK)
+            nc.sync.dma_start(out=raws[pair][:, c0:c1], in_=rows[:, 2 * u * T + c0 : 2 * u * T + c1])
 
-        w8, w4, gates = [], [], []
-        for g, (e0, e1) in enumerate(RUNS):
-            w8.append(keep.tile([P, e1 - e0, 4 * N], U8, name="w8_%d" % g, align_bytes=64))
-            w4.append(keep.tile([P, e1 - e0, 2 * N], U8, name="w4_%d" % g, align_bytes=64))
-        picked = keep.tile([P, PAIRS, 5 * C], U32, name="picked", align_bytes=64)
-        late = keep.tile([P, 2, 2 * C], U32, name="late", align_bytes=64)
+        w8, w4 = [], []
+        for g, (e0, e1) in enumerate(WEIGHT_LOADS):
+            w8.append(keep.tile([P, e1 - e0, 4 * N], U8, name="w8_%d" % g, align_bytes=LONG_ROWS))
+            w4.append(keep.tile([P, e1 - e0, 2 * N], U8, name="w4_%d" % g, align_bytes=LONG_ROWS))
         gates = keep.tile([P, S], F32, name="gates")
         gate_columns = keep.tile([P, 2, 3], F32, name="gate_columns")
         identity = keep.tile([P, P], F32, name="identity")
-        first_gate = late[:].rearrange("p u s -> p (u s)")[:, 3 * C // 2 : 5 * C // 2].bitcast(F32)
-        w8_planes = [keep.tile([P, N], U8, name="w8_plane%d" % h, align_bytes=64) for h in range(2)]
-        w4_plane = keep.tile([P, E, N], U8, name="w4_plane", align_bytes=64)
+        w8_planes = [keep.tile([P, N], U8, name="w8_plane%d" % h, align_bytes=MX_ALIGN) for h in range(2)]
+        w4_plane = keep.tile([P, E, N], U8, name="w4_plane", align_bytes=MX_ALIGN)
 
         def w8_row(e):
             return 4 * e if e < 4 else 4 * e - 8
@@ -82,44 +82,49 @@ def tile_moe_pln_lin_none_kernel(tc, xT, w8_words, w8_scales, w4_words, w4_scale
                     in_=w8_scales[e0:e1, 0, 4 * q : 4 * q + 4, :].bitcast(I32),
                 )
 
-        def load_w4_scales(e0, e1):
-            for r in range(4):
+        def load_w4_scales(e0, e1, residues):
+            for r in residues:
                 nc.sync.dma_start(
                     out=w4_plane[r:P:32, e0:e1, :].bitcast(I32),
                     in_=w4_scales[e0:e1, 0, r:16:4, :].rearrange("e q n -> q e n").bitcast(I32),
                 )
 
-        def load_weights(g):
-            es = slice(RUNS[g][0], RUNS[g][1])
-            nc.sync.dma_start(out=w8[g][:].bitcast(I32), in_=w8_words[es, 0].rearrange("e p n r -> p e (n r)").bitcast(I32))
-            nc.sync.dma_start(out=w4[g][:].bitcast(I32), in_=w4_words[es, 0].rearrange("e p b -> p e b").bitcast(I32))
+        def load_w8(g):
+            e0, e1 = WEIGHT_LOADS[g]
+            nc.sync.dma_start(out=w8[g][:].bitcast(I32), in_=w8_words[e0:e1, 0].rearrange("e p n r -> p e (n r)").bitcast(I32))
 
-        def gate_of(e0, e1):
-            return first_gate if e0 == 0 else gates[:, e0 * C : e1 * C]
+        def load_w4(g):
+            e0, e1 = WEIGHT_LOADS[g]
+            nc.sync.dma_start(out=w4[g][:].bitcast(I32), in_=w4_words[e0:e1, 0].rearrange("e p b -> p e b").bitcast(I32))
 
-        load_x(0)
         nc.sync.dma_start(out=gate_columns[:], in_=gate[0, :].rearrange("(h c x) -> c h x", h=2, x=3))
+        load_x(0, 0, 2 * T)
         nc.sync.dma_start(offsets[:], offs)
-        load_x(1)
+        load_x(1, 0, T + MIDDLE_CUT)
+        load_x(1, T + MIDDLE_CUT, 2 * T)
         load_w8_scales(0)
-        load_x(2)
-        load_x(3)
-        load_x(4)
-        load_weights(0)
-        load_w4_scales(0, 2)
-        load_weights(1)
-        load_w4_scales(2, E)
-        load_weights(2)
-        load_weights(3)
+        load_x(2, 0, T + MIDDLE_CUT)
+        load_w4_scales(0, 2, range(1))
+        load_x(2, T + MIDDLE_CUT, 2 * T)
+        load_x(3, T, 2 * T)
+        load_x(3, LAST_CUT, T)
+        load_x(3, 0, LAST_CUT)
+        load_w4_scales(0, 2, range(1, 4))
+        for g in range(2):
+            load_w8(g)
+            load_w4(g)
+        load_w4_scales(2, E, range(4))
+        load_w8(2)
         load_w8_scales(1)
+        load_w4(2)
 
         windows = []
         for m in range(N_BLOCKS):
-            windows.append(keep.tile([P, T], F32, name="window%d" % m))
+            windows.append(keep.tile([P, T], F32, name="window%d" % m, align_bytes=LONG_ROWS))
             if m < N_BLOCKS - 1:
                 nc.vector.memset(windows[m][:], 0.0)
             else:
-                nc.scalar.copy(out=windows[m][:], in_=windows[0][:])
+                nc.scalar.activation(windows[m][:], windows[0][:], COPY)
 
         make_identity(nc, identity[:])
         for h in range(2):
@@ -128,177 +133,195 @@ def tile_moe_pln_lin_none_kernel(tc, xT, w8_words, w8_scales, w4_words, w4_scale
                 nc.tensor.transpose(spread[:, x, :], gate_columns[:, h, x : x + 1].to_broadcast([P, P]), identity[:])
             half = gates[:, h * S // 2 : (h + 1) * S // 2]
             nc.scalar.copy(out=half.rearrange("p (c x) -> p c x", x=3), in_=spread[:].rearrange("p x c -> p c x"))
-        nc.scalar.copy(out=first_gate, in_=gates[:, 0:C])
 
-        pairs = [keep.tile([P, T], U32, name="pair%d" % u, align_bytes=64) for u in range(PAIRS)]
+        pairs = [keep.tile([P, T], U32, name="pair%d" % u, align_bytes=MX_ALIGN) for u in range(PAIRS)]
+        picked = keep.tile([P, PAIRS, (E - 2) * C], U32, name="picked", align_bytes=MX_ALIGN)
+        last_row = keep.tile([P, C], F32, name="last_row")
 
-        pieces = [(0, 0, 1), (1, 0, 1), (0, 1, 2), (1, 1, 2), (0, 2, 4), (1, 2, 4), (0, 4, 6), (1, 4, 6)]
-        woven_at = {(0, 2, 4): 2048, (0, 4, 6): 4096, (1, 2, 4): 0, (1, 4, 6): 12288}
-        codes_at = {(1, 0, 1): 8192, (1, 2, 4): 7680, (0, 4, 6): 9216}
-        woven, codes, planes, piece_of = {}, {}, {}, {}
-        second = shared.tile([P, PASSES * C, 2], U32, name="woven_second", offset=0, align_bytes=64)
-        second_codes = shared.tile([P, PASSES * C], U32, name="codes_second", offset=8448, align_bytes=64)
-        second_plane = shared.tile([P, PASSES * C], U8, name="plane_second", offset=12288, align_bytes=64)
-        woven[1], codes[1], planes[1] = second[:], second_codes[:], second_plane[:]
-        for piece in pieces:
-            a, e0, e1 = piece
-            n = (e1 - e0) * C
-            for e in range(e0, e1):
-                piece_of[a, e] = piece
-            if e0 == 1:
-                cols = slice(a * C, (a + 1) * C)
-                woven[piece], codes[piece], planes[piece] = second[:, cols, :], second_codes[:, cols], second_plane[:, cols]
-                continue
-            if piece == (1, 0, 1):
-                woven[piece] = picked[:, 3, C : 3 * C].rearrange("p (s u) -> p s u", u=2)
-            elif piece in woven_at:
-                woven[piece] = shared.tile([P, n, 2], U32, name="woven%d%d" % (a, e0), offset=woven_at[piece], align_bytes=64)[:]
+        pieces = [((0, 1), 0, 1), ((0,), 1, 2), ((0,), 2, 4), ((1,), 1, 2), ((1,), 2, 4), ((0,), 4, 6), ((1,), 4, 6)]
+        woven_at = {0: 8192, 2: 0, 4: 10240, 5: 0, 6: 10240}
+        codes_at = {1: 8192, 2: 8704, 4: 13312, 5: 12800, 6: 13824}
+        second_gate = shared.tile([P, C], F32, name="second_gate", offset=13312, align_bytes=MX_ALIGN)
+        woven, codes, planes, piece_of = [], [], [], {}
+        for i, (passes, e0, e1) in enumerate(pieces):
+            shape = [P, len(passes), (e1 - e0) * C]
+            for a in passes:
+                for e in range(e0, e1):
+                    piece_of[a, e] = i
+            if i in woven_at:
+                woven.append(shared.tile(shape + [2], U32, name="woven%d" % i, offset=woven_at[i], align_bytes=MX_ALIGN)[:])
             else:
-                woven[piece] = keep.tile([P, n, 2], U32, name="woven%d%d" % (a, e0), align_bytes=64)[:]
-            if piece in codes_at:
-                codes[piece] = shared.tile([P, n], U32, name="codes%d%d" % (a, e0), offset=codes_at[piece], align_bytes=64)[:]
+                woven.append(keep.tile(shape + [2], U32, name="woven%d" % i, align_bytes=MX_ALIGN)[:])
+            if i in codes_at:
+                codes.append(shared.tile(shape, U32, name="codes%d" % i, offset=codes_at[i], align_bytes=MX_ALIGN)[:])
             else:
-                codes[piece] = keep.tile([P, n], U32, name="codes%d%d" % (a, e0), align_bytes=64)[:]
-            planes[piece] = keep.tile([P, n], U8, name="plane%d%d" % (a, e0), align_bytes=64)[:]
+                codes.append(keep.tile(shape, U32, name="codes%d" % i, align_bytes=MX_ALIGN)[:])
+            planes.append(keep.tile(shape, U8, name="plane%d" % i, align_bytes=MX_ALIGN)[:])
 
-        def round_pair(i):
-            pair, t0, width, share = LOADS[i]
-            halves = pairs[pair][:, t0 : t0 + width].bitcast(BF16).rearrange("p (t e) -> p t e", e=2)
-            first, rest = slice(0, share), slice(share, width)
-            nc.scalar.copy(
-                out=halves[:, first, :].rearrange("p (c i) e -> p c e i", i=4),
-                in_=raws[i][:, :, first].rearrange("p e (c i) -> p c e i", i=4),
-            )
-            if i == 0:
-                nc.vector.tensor_copy(
-                    out=halves[:, rest, :].rearrange("p (c i) e -> p c e i", i=4),
-                    in_=raws[i][:, :, rest].rearrange("p e (c i) -> p c e i", i=4),
-                )
-            else:
-                nc.gpsimd.tensor_copy(out=halves[:, rest, :], in_=raws[i][:, :, rest].rearrange("p e t -> p t e"))
+        gate_copies = {
+            (0, 1): woven[3][:, 0, :, 1].bitcast(F32),
+            (0, 2): picked[:, 3, 3 * C // 2 : 5 * C // 2].bitcast(F32),
+            (1, 1): second_gate[:],
+        }
 
-        def picked_rows(a, e0, e1):
-            if (a, e0) == (1, 4):
-                return late[:]
-            return picked[:, 2 * a : 2 * a + 2, (e0 - 1) * C : (e1 - 1) * C]
+        def round_pair(pair, t0, t1, engine):
+            halves = pairs[pair][:, t0:t1].bitcast(BF16).rearrange("p (t e) -> p t e", e=2)
+            rows = raws[pair][:].rearrange("p (e t) -> p e t", e=2)[:, :, t0:t1]
+            if engine == "gpsimd":
+                nc.gpsimd.tensor_copy(out=halves, in_=rows.rearrange("p e t -> p t e"))
+                return
+            copy = nc.scalar.copy if engine == "scalar" else nc.vector.tensor_copy
+            copy(out=halves.rearrange("p (c i) e -> p c e i", i=4), in_=rows.rearrange("p e (c i) -> p c e i", i=4))
 
         def gather(pair, e0, e1):
-            nc.vector.tensor_copy(picked_rows(pair // 2, e0, e1)[:, pair % 2, :], pairs[pair][:].indirect(listed(e0 * C, e1 * C)))
+            nc.vector.tensor_copy(picked[:, pair, (e0 - 2) * C : (e1 - 2) * C], pairs[pair][:].indirect(listed(e0 * C, e1 * C)))
 
-        def gather_woven(pair, e0, e1):
+        def gather_woven(pair, e):
             a, u = divmod(pair, 2)
-            nc.vector.tensor_copy(woven[a, e0, e1][:, :, u], pairs[pair][:].indirect(listed(e0 * C, e1 * C)))
+            i = piece_of[a, e]
+            nc.vector.tensor_copy(woven[i][:, pieces[i][0].index(a), :, u], pairs[pair][:].indirect(listed(e * C, (e + 1) * C)))
 
-        def weave(a, e0, e1, engine):
-            piece = piece_of[a, e0]
-            two = picked_rows(a, e0, e1)
-            both = woven[piece][:, (e0 - piece[1]) * C : (e1 - piece[1]) * C, :]
-            if engine == "vector":
-                nc.vector.tensor_copy(
-                    out=both.bitcast(I32).rearrange("p (c i) u -> p c u i", i=4),
-                    in_=two.bitcast(I32).rearrange("p u (c i) -> p c u i", i=4),
-                )
-            elif engine == "scalar":
-                nc.scalar.copy(out=both.rearrange("p (c i) u -> p c u i", i=4), in_=two.rearrange("p u (c i) -> p c u i", i=4))
-            else:
-                nc.gpsimd.tensor_copy(out=both, in_=two.rearrange("p u s -> p s u"))
+        def weave(i):
+            passes, e0, e1 = pieces[i]
+            rows = picked[:, 2 * passes[0] : 2 * passes[-1] + 2, (e0 - 2) * C : (e1 - 2) * C]
+            nc.gpsimd.tensor_copy(out=woven[i], in_=rows.rearrange("p (a u) s -> p a s u", u=2))
 
-        def quantise(piece):
-            values = woven[piece].rearrange("p s u -> p (s u)").bitcast(BF16)
-            nc.vector.quantize_mx(out=codes[piece].bitcast(FP8X4), scales=planes[piece], in_=values)
+        def quantise(i):
+            values = woven[i].rearrange("p a s u -> p (a s u)").bitcast(BF16)
+            nc.vector.quantize_mx(
+                out=codes[i].rearrange("p a s -> p (a s)").bitcast(FP8X4),
+                scales=planes[i].rearrange("p a s -> p (a s)"),
+                in_=values,
+            )
 
-        def product(acc, e, m, a):
-            g = [h for h in range(len(RUNS)) if RUNS[h][0] <= e][-1]
-            i = e - RUNS[g][0]
-            piece = piece_of[a, e]
-            cols = slice((e - piece[1]) * C, (e - piece[1] + 1) * C)
+        def product(acc, e, m, a, start, stop):
+            g = [h for h in range(len(WEIGHT_LOADS)) if WEIGHT_LOADS[h][0] <= e][-1]
+            j = e - WEIGHT_LOADS[g][0]
+            i = piece_of[a, e]
+            passes, e0, e1 = pieces[i]
+            cols = slice((e - e0) * C, (e - e0 + 1) * C)
             if a == 0:
-                w_codes = w8[g][:, i, 4 * P * m : 4 * P * (m + 1)].bitcast(FP8X4)
+                w_codes = w8[g][:, j, 4 * P * m : 4 * P * (m + 1)].bitcast(FP8X4)
                 w_scale = w8_planes[e // 4][w8_row(e) :, P * m : P * (m + 1)]
             else:
-                w_codes = w4[g][:, i, 2 * P * m : 2 * P * (m + 1)].bitcast(FP4X4)
+                w_codes = w4[g][:, j, 2 * P * m : 2 * P * (m + 1)].bitcast(FP4X4)
                 w_scale = w4_plane[:, e, P * m : P * (m + 1)]
             nc.tensor.matmul_mx(
                 out=acc,
                 lhsT=w_codes,
                 lhsT_scale=w_scale,
-                rhs=codes[piece][:, cols].bitcast(FP8X4),
-                rhs_scale=planes[piece][:, cols],
-                start=(a == 0),
-                stop=(a == PASSES - 1),
+                rhs=codes[i][:, passes.index(a), cols].bitcast(FP8X4),
+                rhs_scale=planes[i][:, passes.index(a), cols],
+                start=start,
+                stop=stop,
             )
 
-        results = keep.tile([P, N_BLOCKS, S], F32, name="results")
-        rows = {1: 0, 2: 1, 0: 2}
+        results = keep.tile([P, N_BLOCKS * S], F32, name="results")
+        units = [(1, e) for e in range(E)] + [(2, 0), (0, 0), (2, 1)] + [(0, e) for e in range(1, E)] + [(2, e) for e in range(2, E)]
 
-        def multiply(e0, e1, blocks, bank):
-            acc = psum.tile([P, len(blocks), (e1 - e0) * C], F32, name="acc%d_%d" % (e0, blocks[0]), tag="bank%d" % bank)
-            for b, m in enumerate(blocks):
-                for e in range(e0, e1):
-                    for a in range(PASSES):
-                        product(acc[:, b, (e - e0) * C : (e - e0 + 1) * C], e, m, a)
-            return acc
+        def result_columns(m, s0, count):
+            at = units.index((m, s0 // C)) * C + s0 % C
+            return results[:, at : at + count]
+
+        def sums(e0, e1, blocks, bank):
+            return psum.tile([P, len(blocks), (e1 - e0) * C], F32, name="acc%d_%d" % (e0, blocks[0]), tag="bank%d" % bank)
+
+        def multiply(acc, e0, e1, blocks, a):
+            parts = [(b, m, e) for b, m in enumerate(blocks) for e in range(e0, e1)]
+            for b, m, e in parts:
+                start = a == 0 and (b, m, e) == parts[0]
+                stop = a == PASSES - 1 and (b, m, e) == parts[-1]
+                product(acc[:, b, (e - e0) * C : (e - e0 + 1) * C], e, m, a, start, stop)
 
         def empty(acc, e0, e1, blocks):
             n = (e1 - e0) * C
-            r = rows[blocks[0]]
             nc.vector.tensor_tensor(
-                results[:, r : r + len(blocks), e0 * C : e1 * C],
+                result_columns(blocks[0], e0 * C, len(blocks) * n).rearrange("p (b s) -> p b s", s=n),
                 acc[:],
-                gate_of(e0, e1).unsqueeze(1).to_broadcast([P, len(blocks), n]),
+                gate_copies.get((e0, blocks[0]), gates[:, e0 * C : e1 * C]).unsqueeze(1).to_broadcast([P, len(blocks), n]),
                 MULT,
             )
 
         def scatter(s0, s1, m, on_scalar):
-            values = results[:, rows[m], s0:s1]
+            values = result_columns(m, s0, s1 - s0)
             if on_scalar:
                 nc.scalar.activation(windows[m][:].indirect(listed(s0, s1)), values, COPY)
             else:
                 nc.vector.tensor_copy(windows[m][:].indirect(listed(s0, s1)), values)
 
-        for pair in range(2):
-            round_pair(pair)
-            gather(pair, 1, E)
-            gather_woven(pair, 0, 1)
-        quantise((0, 0, 1))
-        round_pair(2)
-        round_pair(3)
-        gather(2, 1, 4)
-        gather_woven(2, 0, 1)
-        round_pair(4)
-        weave(0, 2, 4, "scalar")
-        weave(0, 1, 2, "scalar")
-        weave(0, 4, 6, "gpsimd")
-        gather_woven(3, 0, 1)
-        gather(3, 1, 2)
-        weave(1, 1, 2, "scalar")
-        quantise((1, 0, 1))
-        quantise((0, 2, 4))
+        round_pair(0, 0, FIRST_SHARE, "scalar")
+        round_pair(0, FIRST_SHARE, T, "vector")
+        for (e, m), copy_of_gate in gate_copies.items():
+            nc.scalar.copy(out=copy_of_gate, in_=gates[:, e * C : (e + 1) * C])
+        gather(0, 2, E)
+        gather_woven(0, 0)
+        gather_woven(0, 1)
+        for pair in (1, 2):
+            round_pair(pair, 0, MIDDLE_SHARES[0], "scalar")
+            round_pair(pair, MIDDLE_SHARES[0], MIDDLE_CUT, "gpsimd")
+            round_pair(pair, MIDDLE_CUT, MIDDLE_SHARES[1], "scalar")
+            round_pair(pair, MIDDLE_SHARES[1], T, "gpsimd")
+            if pair == 1:
+                gather(1, 2, E)
+                gather_woven(1, 0)
+                gather_woven(1, 1)
+        gather_woven(2, 0)
+        gather_woven(2, 1)
+        gather(2, 2, E)
+        weave(2)
+
+        first_values = woven[0][:, 1].rearrange("p s u -> p (s u)").bitcast(BF16)
+        nc.scalar.activation(last_row[:], raws[3][:, T : 2 * T].indirect(listed(0, C)), COPY)
+        nc.scalar.copy(out=first_values[:, 3 : PACK * C : PACK], in_=last_row[:])
+        nc.scalar.activation(first_values[:, 2 : PACK * C : PACK], raws[3][:].indirect(listed(0, C)), COPY)
+        round_pair(3, LAST_SHARE, T, "gpsimd")
+        round_pair(3, 0, LAST_SHARE, "scalar")
+        for i in range(3):
+            quantise(i)
+        banks = {0: (([1], 0), ([2, 0], 1)), 1: (([1], 2), ([2, 0], 3)), 2: (([1], 4), ([2], 5), ([0], 6)), 3: (([1], 7), ([2], 0), ([0], 1))}
+        accs = {}
+
+        def first_passes(g):
+            accs[g] = [sums(RUNS[g][0], RUNS[g][1], blocks, bank) for blocks, bank in banks[g]]
+            for acc, (blocks, bank) in zip(accs[g], banks[g]):
+                multiply(acc, RUNS[g][0], RUNS[g][1], blocks, 0)
+
+        def finish(g, which):
+            for i in which:
+                multiply(accs[g][i], RUNS[g][0], RUNS[g][1], banks[g][i][0], 1)
+                empty(accs[g][i], RUNS[g][0], RUNS[g][1], banks[g][i][0])
+
+        for blocks, bank in banks[0]:
+            acc = sums(0, 1, blocks, bank)
+            for a in range(PASSES):
+                multiply(acc, 0, 1, blocks, a)
+            empty(acc, 0, 1, blocks)
+        weave(5)
+        first_passes(1)
+        gather_woven(3, 1)
+        quantise(3)
         gather(3, 2, 4)
-        for blocks, bank in [([1], 0), ([2, 0], 1)]:
-            empty(multiply(0, 1, blocks, bank), 0, 1, blocks)
-        quantise(1)
-        weave(1, 2, 4, "gpsimd")
-        gather(2, 4, 6)
+        weave(4)
         gather(3, 4, 6)
-        accs = [multiply(1, 2, blocks, bank) for blocks, bank in (([1], 2), ([2, 0], 6))]
-        empty(accs[0], 1, 2, [1])
-        quantise((1, 2, 4))
-        empty(accs[1], 1, 2, [2, 0])
-        for e, m in [(0, 1), (0, 2), (0, 0), (1, 1), (1, 2)]:
+        finish(1, range(2))
+        first_passes(2)
+        quantise(4)
+        weave(6)
+        for e, m in [(0, 1), (0, 0), (0, 2), (1, 1), (1, 2)]:
             scatter(e * C, (e + 1) * C, m, True)
-        weave(1, 4, 6, "vector")
-        quantise((0, 4, 6))
-        for m in (1, 0, 2):
-            empty(multiply(2, 4, [m], 3 + m), 2, 4, [m])
-            if m == 1:
-                quantise((1, 4, 6))
+        scatter(C, 2 * C, 0, False)
+        finish(2, range(2))
+        multiply(accs[2][2], 2, 4, [0], 1)
+        quantise(5)
+        first_passes(3)
+        quantise(6)
+        empty(accs[2][2], 2, 4, [0])
         scatter(2 * C, 4 * C, 1, True)
         scatter(2 * C, 3 * C, 2, True)
-        scatter(C, CUT, 0, False)
-        for m, bank in ((1, 7), (0, 0), (2, 1)):
-            empty(multiply(4, 6, [m], bank), 4, 6, [m])
-        for m in (1, 0, 2):
-            scatter({1: 4 * C, 0: CUT, 2: 3 * C}[m], S, m, m > 0)
+        scatter(2 * C, 3 * C, 0, False)
+        finish(3, range(3))
+        scatter(4 * C, S, 1, True)
+        scatter(3 * C, S, 0, False)
+        scatter(3 * C, S, 2, True)
         for m in (1, 0, 2):
             nc.sync.dma_start(out=out[m * P : (m + 1) * P, :], in_=windows[m][:])

@@ -34,7 +34,7 @@ FIRST_SHARE = 384
 MIDDLE_CUT = 448
 MIDDLE_SHARES = (240, 768)
 LAST_CUT = 512
-LAST_SHARE = 656
+LAST_SHARE = 688
 
 
 def tile_moe_pln_lin_none_kernel(tc, xT, w8_words, w8_scales, w4_words, w4_scales, gate, offs, out):
@@ -132,15 +132,16 @@ def tile_moe_pln_lin_none_kernel(tc, xT, w8_words, w8_scales, w4_words, w4_scale
             for x in range(3):
                 nc.tensor.transpose(spread[:, x, :], gate_columns[:, h, x : x + 1].to_broadcast([P, P]), identity[:])
             half = gates[:, h * S // 2 : (h + 1) * S // 2]
-            nc.scalar.copy(out=half.rearrange("p (c x) -> p c x", x=3), in_=spread[:].rearrange("p x c -> p c x"))
+            copy = nc.vector.tensor_copy if h == 0 else nc.scalar.copy
+            copy(out=half.rearrange("p (c x) -> p c x", x=3), in_=spread[:].rearrange("p x c -> p c x"))
 
         pairs = [keep.tile([P, T], U32, name="pair%d" % u, align_bytes=MX_ALIGN) for u in range(PAIRS)]
         picked = keep.tile([P, PAIRS, (E - 2) * C], U32, name="picked", align_bytes=MX_ALIGN)
         last_row = keep.tile([P, C], F32, name="last_row")
 
-        pieces = [((0, 1), 0, 1), ((0,), 1, 2), ((0,), 2, 4), ((1,), 1, 2), ((1,), 2, 4), ((0,), 4, 6), ((1,), 4, 6)]
-        woven_at = {0: 8192, 2: 0, 4: 10240, 5: 0, 6: 10240}
-        codes_at = {1: 8192, 2: 8704, 4: 13312, 5: 12800, 6: 13824}
+        pieces = [((0,), 0, 2), ((1,), 0, 1), ((0,), 2, 4), ((1,), 1, 2), ((1,), 2, 4), ((0,), 4, 6), ((1,), 4, 6)]
+        woven_at = {1: 8192, 2: 0, 4: 10240, 5: 0, 6: 10240}
+        codes_at = {2: 8192, 4: 13312, 5: 12800, 6: 13824}
         second_gate = shared.tile([P, C], F32, name="second_gate", offset=13312, align_bytes=MX_ALIGN)
         woven, codes, planes, piece_of = [], [], [], {}
         for i, (passes, e0, e1) in enumerate(pieces):
@@ -164,6 +165,9 @@ def tile_moe_pln_lin_none_kernel(tc, xT, w8_words, w8_scales, w4_words, w4_scale
             (1, 1): second_gate[:],
         }
 
+        for (e, m), copy_of_gate in gate_copies.items():
+            nc.vector.tensor_copy(out=copy_of_gate, in_=gates[:, e * C : (e + 1) * C])
+
         def round_pair(pair, t0, t1, engine):
             halves = pairs[pair][:, t0:t1].bitcast(BF16).rearrange("p (t e) -> p t e", e=2)
             rows = raws[pair][:].rearrange("p (e t) -> p e t", e=2)[:, :, t0:t1]
@@ -176,10 +180,9 @@ def tile_moe_pln_lin_none_kernel(tc, xT, w8_words, w8_scales, w4_words, w4_scale
         def gather(pair, e0, e1):
             nc.vector.tensor_copy(picked[:, pair, (e0 - 2) * C : (e1 - 2) * C], pairs[pair][:].indirect(listed(e0 * C, e1 * C)))
 
-        def gather_woven(pair, e):
-            a, u = divmod(pair, 2)
-            i = piece_of[a, e]
-            nc.vector.tensor_copy(woven[i][:, pieces[i][0].index(a), :, u], pairs[pair][:].indirect(listed(e * C, (e + 1) * C)))
+        def gather_woven(pair, i):
+            passes, e0, e1 = pieces[i]
+            nc.vector.tensor_copy(woven[i][:, 0, :, pair % 2], pairs[pair][:].indirect(listed(e0 * C, e1 * C)))
 
         def weave(i):
             passes, e0, e1 = pieces[i]
@@ -251,11 +254,8 @@ def tile_moe_pln_lin_none_kernel(tc, xT, w8_words, w8_scales, w4_words, w4_scale
 
         round_pair(0, 0, FIRST_SHARE, "scalar")
         round_pair(0, FIRST_SHARE, T, "vector")
-        for (e, m), copy_of_gate in gate_copies.items():
-            nc.scalar.copy(out=copy_of_gate, in_=gates[:, e * C : (e + 1) * C])
         gather(0, 2, E)
         gather_woven(0, 0)
-        gather_woven(0, 1)
         for pair in (1, 2):
             round_pair(pair, 0, MIDDLE_SHARES[0], "scalar")
             round_pair(pair, MIDDLE_SHARES[0], MIDDLE_CUT, "gpsimd")
@@ -264,19 +264,19 @@ def tile_moe_pln_lin_none_kernel(tc, xT, w8_words, w8_scales, w4_words, w4_scale
             if pair == 1:
                 gather(1, 2, E)
                 gather_woven(1, 0)
-                gather_woven(1, 1)
-        gather_woven(2, 0)
+                quantise(0)
         gather_woven(2, 1)
+        gather_woven(2, 3)
         gather(2, 2, E)
         weave(2)
 
-        first_values = woven[0][:, 1].rearrange("p s u -> p (s u)").bitcast(BF16)
+        first_values = woven[1][:, 0].rearrange("p s u -> p (s u)").bitcast(BF16)
         nc.scalar.activation(last_row[:], raws[3][:, T : 2 * T].indirect(listed(0, C)), COPY)
         nc.scalar.copy(out=first_values[:, 3 : PACK * C : PACK], in_=last_row[:])
         nc.scalar.activation(first_values[:, 2 : PACK * C : PACK], raws[3][:].indirect(listed(0, C)), COPY)
         round_pair(3, LAST_SHARE, T, "gpsimd")
         round_pair(3, 0, LAST_SHARE, "scalar")
-        for i in range(3):
+        for i in (1, 2):
             quantise(i)
         banks = {0: (([1], 0), ([2, 0], 1)), 1: (([1], 2), ([2, 0], 3)), 2: (([1], 4), ([2], 5), ([0], 6)), 3: (([1], 7), ([2], 0), ([0], 1))}
         accs = {}
@@ -298,7 +298,7 @@ def tile_moe_pln_lin_none_kernel(tc, xT, w8_words, w8_scales, w4_words, w4_scale
             empty(acc, 0, 1, blocks)
         weave(5)
         first_passes(1)
-        gather_woven(3, 1)
+        gather_woven(3, 3)
         quantise(3)
         gather(3, 2, 4)
         weave(4)

@@ -35,6 +35,7 @@ MIDDLE_CUT = 448
 MIDDLE_SHARES = (240, 768)
 LAST_CUT = 512
 LAST_SHARE = 688
+HANDED_BACK = 3 * C + 32
 
 
 def tile_moe_pln_lin_none_kernel(tc, xT, w8_words, w8_scales, w4_words, w4_scales, gate, offs, out):
@@ -140,8 +141,8 @@ def tile_moe_pln_lin_none_kernel(tc, xT, w8_words, w8_scales, w4_words, w4_scale
         last_row = keep.tile([P, C], F32, name="last_row")
 
         pieces = [((0,), 0, 2), ((1,), 0, 1), ((0,), 2, 4), ((1,), 1, 2), ((1,), 2, 4), ((0,), 4, 6), ((1,), 4, 6)]
-        woven_at = {1: 8192, 2: 0, 4: 10240, 5: 0, 6: 10240}
-        codes_at = {2: 8192, 4: 13312, 5: 12800, 6: 13824}
+        woven_at = {1: 8192, 2: 0, 4: 10240, 5: 0, 6: 0}
+        codes_at = {2: 8192, 4: 13312, 5: 10240, 6: 13824}
         second_gate = shared.tile([P, C], F32, name="second_gate", offset=13312, align_bytes=MX_ALIGN)
         woven, codes, planes, piece_of = [], [], [], {}
         for i, (passes, e0, e1) in enumerate(pieces):
@@ -262,8 +263,8 @@ def tile_moe_pln_lin_none_kernel(tc, xT, w8_words, w8_scales, w4_words, w4_scale
             round_pair(pair, MIDDLE_CUT, MIDDLE_SHARES[1], "scalar")
             round_pair(pair, MIDDLE_SHARES[1], T, "gpsimd")
             if pair == 1:
-                gather(1, 2, E)
                 gather_woven(1, 0)
+                gather(1, 2, E)
                 quantise(0)
         gather_woven(2, 1)
         gather_woven(2, 3)
@@ -278,7 +279,7 @@ def tile_moe_pln_lin_none_kernel(tc, xT, w8_words, w8_scales, w4_words, w4_scale
         round_pair(3, 0, LAST_SHARE, "scalar")
         for i in (1, 2):
             quantise(i)
-        banks = {0: (([1], 0), ([2, 0], 1)), 1: (([1], 2), ([2, 0], 3)), 2: (([1], 4), ([2], 5), ([0], 6)), 3: (([1], 7), ([2], 0), ([0], 1))}
+        banks = {0: (([1], 0), ([2, 0], 1)), 1: (([1], 2), ([2, 0], 3)), 2: (([1], 4), ([2], 5), ([0], 6)), 3: (([1], 7), ([0], 0), ([2], 1))}
         accs = {}
 
         def first_passes(g):
@@ -306,22 +307,21 @@ def tile_moe_pln_lin_none_kernel(tc, xT, w8_words, w8_scales, w4_words, w4_scale
         finish(1, range(2))
         first_passes(2)
         quantise(4)
-        weave(6)
-        for e, m in [(0, 1), (0, 0), (0, 2), (1, 1), (1, 2)]:
-            scatter(e * C, (e + 1) * C, m, True)
-        scatter(C, 2 * C, 0, False)
-        finish(2, range(2))
-        multiply(accs[2][2], 2, 4, [0], 1)
         quantise(5)
-        first_passes(3)
+        weave(6)
+        for e, m in [(0, 1), (0, 0), (0, 2), (1, 1), (1, 2), (1, 0)]:
+            scatter(e * C, (e + 1) * C, m, True)
+        finish(2, range(3))
         quantise(6)
-        empty(accs[2][2], 2, 4, [0])
         scatter(2 * C, 4 * C, 1, True)
-        scatter(2 * C, 3 * C, 2, True)
-        scatter(2 * C, 3 * C, 0, False)
-        finish(3, range(3))
+        scatter(2 * C, HANDED_BACK, 2, False)
+        for blocks, bank in banks[3]:
+            acc = sums(4, 6, blocks, bank)
+            for a in range(PASSES):
+                multiply(acc, 4, 6, blocks, a)
+            empty(acc, 4, 6, blocks)
         scatter(4 * C, S, 1, True)
-        scatter(3 * C, S, 0, False)
-        scatter(3 * C, S, 2, True)
+        scatter(2 * C, S, 0, False)
+        scatter(HANDED_BACK, S, 2, True)
         for m in (1, 0, 2):
             nc.sync.dma_start(out=out[m * P : (m + 1) * P, :], in_=windows[m][:])

@@ -263,8 +263,8 @@ def tile_moe_pln_lin_none_kernel(tc, xT, w8_words, w8_scales, w4_words, w4_scale
             round_pair(pair, MIDDLE_CUT, MIDDLE_SHARES[1], "scalar")
             round_pair(pair, MIDDLE_SHARES[1], T, "gpsimd")
             if pair == 1:
-                gather_woven(1, 0)
                 gather(1, 2, E)
+                gather_woven(1, 0)
                 quantise(0)
         gather_woven(2, 1)
         gather_woven(2, 3)

@@ -105,12 +105,11 @@ def tile_moe_pln_lin_none_kernel(tc, xT, w8_words, w8_scales, w4_words, w4_scale
         load_x(1, T + MIDDLE_CUT, 2 * T)
         load_w8_scales(0)
         load_x(2, 0, T + MIDDLE_CUT)
-        load_w4_scales(0, 2, range(1))
         load_x(2, T + MIDDLE_CUT, 2 * T)
         load_x(3, T, 2 * T)
         load_x(3, LAST_CUT, T)
         load_x(3, 0, LAST_CUT)
-        load_w4_scales(0, 2, range(1, 4))
+        load_w4_scales(0, 2, range(4))
         for g in range(2):
             load_w8(g)
             load_w4(g)
@@ -140,9 +139,9 @@ def tile_moe_pln_lin_none_kernel(tc, xT, w8_words, w8_scales, w4_words, w4_scale
         picked = keep.tile([P, PAIRS, (E - 2) * C], U32, name="picked", align_bytes=MX_ALIGN)
         last_row = keep.tile([P, C], F32, name="last_row")
 
-        pieces = [((0,), 0, 2), ((1,), 0, 1), ((0,), 2, 4), ((1,), 1, 2), ((1,), 2, 4), ((0,), 4, 6), ((1,), 4, 6)]
+        pieces = [((0,), 0, 1), ((1,), 0, 1), ((0,), 2, 4), ((1,), 1, 2), ((1,), 2, 4), ((0,), 4, 6), ((1,), 4, 6), ((0,), 1, 2)]
         woven_at = {1: 8192, 2: 0, 4: 10240, 5: 0, 6: 0}
-        codes_at = {2: 8192, 4: 13312, 5: 10240, 6: 13824}
+        codes_at = {7: 8192, 2: 8704, 4: 13312, 5: 10240, 6: 13824}
         second_gate = shared.tile([P, C], F32, name="second_gate", offset=13312, align_bytes=MX_ALIGN)
         woven, codes, planes, piece_of = [], [], [], {}
         for i, (passes, e0, e1) in enumerate(pieces):
@@ -257,6 +256,7 @@ def tile_moe_pln_lin_none_kernel(tc, xT, w8_words, w8_scales, w4_words, w4_scale
         round_pair(0, FIRST_SHARE, T, "vector")
         gather(0, 2, E)
         gather_woven(0, 0)
+        gather_woven(0, 7)
         for pair in (1, 2):
             round_pair(pair, 0, MIDDLE_SHARES[0], "scalar")
             round_pair(pair, MIDDLE_SHARES[0], MIDDLE_CUT, "gpsimd")
@@ -265,6 +265,7 @@ def tile_moe_pln_lin_none_kernel(tc, xT, w8_words, w8_scales, w4_words, w4_scale
             if pair == 1:
                 gather(1, 2, E)
                 gather_woven(1, 0)
+                gather_woven(1, 7)
                 quantise(0)
         gather_woven(2, 1)
         gather_woven(2, 3)
@@ -272,12 +273,15 @@ def tile_moe_pln_lin_none_kernel(tc, xT, w8_words, w8_scales, w4_words, w4_scale
         weave(2)
 
         first_values = woven[1][:, 0].rearrange("p s u -> p (s u)").bitcast(BF16)
-        nc.scalar.activation(last_row[:], raws[3][:, T : 2 * T].indirect(listed(0, C)), COPY)
-        nc.scalar.copy(out=first_values[:, 3 : PACK * C : PACK], in_=last_row[:])
+        halves = (slice(0, C // 2), slice(C // 2, C))
+        for half in halves:
+            nc.scalar.activation(last_row[:, half], raws[3][:, T : 2 * T].indirect(listed(half.start, half.stop)), COPY)
+        for half in halves:
+            nc.scalar.copy(out=first_values[:, PACK * half.start + 3 : PACK * half.stop : PACK], in_=last_row[:, half])
         nc.scalar.activation(first_values[:, 2 : PACK * C : PACK], raws[3][:].indirect(listed(0, C)), COPY)
         round_pair(3, LAST_SHARE, T, "gpsimd")
         round_pair(3, 0, LAST_SHARE, "scalar")
-        for i in (1, 2):
+        for i in (1, 7, 2):
             quantise(i)
         banks = {0: (([1], 0), ([2, 0], 1)), 1: (([1], 2), ([2, 0], 3)), 2: (([1], 4), ([2], 5), ([0], 6)), 3: (([1], 7), ([0], 0), ([2], 1))}
         accs = {}

@@ -32,7 +32,7 @@ BYTES = 4 * K * T + E * N * (4 * P + 2 * P + 2 * 16) + 4 * S + 2 * S + 4 * N * T
 
 FIRST_SHARE = 384
 MIDDLE_CUT = 448
-MIDDLE_SHARES = (240, 768)
+MIDDLE_SHARES = {1: (240, 768), 2: (240, 832)}
 LAST_CUT = 512
 LAST_SHARE = 688
 HANDED_BACK = 3 * C + 32
@@ -105,11 +105,12 @@ def tile_moe_pln_lin_none_kernel(tc, xT, w8_words, w8_scales, w4_words, w4_scale
         load_x(1, T + MIDDLE_CUT, 2 * T)
         load_w8_scales(0)
         load_x(2, 0, T + MIDDLE_CUT)
+        load_w4_scales(0, 2, range(1))
         load_x(2, T + MIDDLE_CUT, 2 * T)
         load_x(3, T, 2 * T)
         load_x(3, LAST_CUT, T)
         load_x(3, 0, LAST_CUT)
-        load_w4_scales(0, 2, range(4))
+        load_w4_scales(0, 2, range(1, 4))
         for g in range(2):
             load_w8(g)
             load_w4(g)
@@ -258,10 +259,11 @@ def tile_moe_pln_lin_none_kernel(tc, xT, w8_words, w8_scales, w4_words, w4_scale
         gather_woven(0, 0)
         gather_woven(0, 7)
         for pair in (1, 2):
-            round_pair(pair, 0, MIDDLE_SHARES[0], "scalar")
-            round_pair(pair, MIDDLE_SHARES[0], MIDDLE_CUT, "gpsimd")
-            round_pair(pair, MIDDLE_CUT, MIDDLE_SHARES[1], "scalar")
-            round_pair(pair, MIDDLE_SHARES[1], T, "gpsimd")
+            early, late = MIDDLE_SHARES[pair]
+            round_pair(pair, 0, early, "scalar")
+            round_pair(pair, early, MIDDLE_CUT, "gpsimd")
+            round_pair(pair, MIDDLE_CUT, late, "scalar")
+            round_pair(pair, late, T, "gpsimd")
             if pair == 1:
                 gather(1, 2, E)
                 gather_woven(1, 0)

from contextlib import ExitStack

import concourse.mybir as mybir
from concourse.masks import make_identity

F32 = mybir.dt.float32
BF16 = mybir.dt.bfloat16
I32 = mybir.dt.int32
U32 = mybir.dt.uint32
U16 = mybir.dt.uint16
U8 = mybir.dt.uint8
FP8X4 = mybir.dt.float8_e4m3fn_x4
FP4X4 = mybir.dt.float4_e2m1fn_x4
MULT = mybir.AluOpType.mult
COPY = mybir.ActivationFunctionType.Copy

P = 128
PACK = 4
K_PASS = P * PACK
K, T, E, C, N = 1024, 1024, 6, 128, 384
S = E * C
N_BLOCKS = N // P
PASSES = K // K_PASS
PAIRS = 4
RUNS = [(0, 1), (1, 2), (2, 4), (4, 6)]
WEIGHT_LOADS = [(0, 1), (1, 4), (4, 6)]
LONG_ROWS = 256
MX_ALIGN = 64

FLOPS = 2 * S * K * N
BYTES = 4 * K * T + E * N * (4 * P + 2 * P + 2 * 16) + 4 * S + 2 * S + 4 * N * T

FIRST_SHARE = 384
MIDDLE_CUT = 448
MIDDLE_SHARES = {1: (240, 768), 2: (240, 832)}
LAST_CUT = 512
LAST_SHARE = 688
HANDED_BACK = 3 * C + 32


def tile_moe_pln_lin_none_kernel(tc, xT, w8_words, w8_scales, w4_words, w4_scales, gate, offs, out):
    nc = tc.nc
    with ExitStack() as ctx:
        keep = ctx.enter_context(tc.tile_pool(name="keep", bufs=1))
        shared = ctx.enter_context(tc.tile_pool(name="shared", bufs=1))
        psum = ctx.enter_context(tc.psum_pool(name="psum", bufs=1))

        offsets = keep.tile([P, S // 16], U16, name="offsets")

        def listed(s0, s1):
            return offsets[:, s0 // 16 : s1 // 16]

        raws = []
        for u in range(PAIRS):
            if u == 2:
                raws.append(shared.tile([P, 2 * T], F32, name="raw2", offset=0, align_bytes=LONG_ROWS))
            else:
                raws.append(keep.tile([P, 2 * T], F32, name="raw%d" % u, align_bytes=LONG_ROWS))

        def load_x(pair, c0, c1):
            a, u = divmod(pair, 2)
            rows = xT[a * K_PASS : (a + 1) * K_PASS, :].rearrange("(p j) t -> p (j t)", j=PACK)
            nc.sync.dma_start(out=raws[pair][:, c0:c1], in_=rows[:, 2 * u * T + c0 : 2 * u * T + c1])

        w8, w4 = [], []
        for g, (e0, e1) in enumerate(WEIGHT_LOADS):
            w8.append(keep.tile([P, e1 - e0, 4 * N], U8, name="w8_%d" % g, align_bytes=LONG_ROWS))
            w4.append(keep.tile([P, e1 - e0, 2 * N], U8, name="w4_%d" % g, align_bytes=LONG_ROWS))
        gates = keep.tile([P, S], F32, name="gates")
        gate_columns = keep.tile([P, 2, 3], F32, name="gate_columns")
        identity = keep.tile([P, P], F32, name="identity")
        w8_planes = [keep.tile([P, N], U8, name="w8_plane%d" % h, align_bytes=MX_ALIGN) for h in range(2)]
        w4_plane = keep.tile([P, E, N], U8, name="w4_plane", align_bytes=MX_ALIGN)

        def w8_row(e):
            return 4 * e if e < 4 else 4 * e - 8

        def load_w8_scales(h):
            e0, e1 = (0, 4) if h == 0 else (4, 6)
            for q in range(4):
                nc.sync.dma_start(
                    out=w8_planes[h][32 * q + w8_row(e0) : 32 * q + 16, :].bitcast(I32),
                    in_=w8_scales[e0:e1, 0, 4 * q : 4 * q + 4, :].bitcast(I32),
                )

        def load_w4_scales(e0, e1, residues):
            for r in residues:
                nc.sync.dma_start(
                    out=w4_plane[r:P:32, e0:e1, :].bitcast(I32),
                    in_=w4_scales[e0:e1, 0, r:16:4, :].rearrange("e q n -> q e n").bitcast(I32),
                )

        def load_w8(g):
            e0, e1 = WEIGHT_LOADS[g]
            nc.sync.dma_start(out=w8[g][:].bitcast(I32), in_=w8_words[e0:e1, 0].rearrange("e p n r -> p e (n r)").bitcast(I32))

        def load_w4(g):
            e0, e1 = WEIGHT_LOADS[g]
            nc.sync.dma_start(out=w4[g][:].bitcast(I32), in_=w4_words[e0:e1, 0].rearrange("e p b -> p e b").bitcast(I32))

        nc.sync.dma_start(out=gate_columns[:], in_=gate[0, :].rearrange("(h c x) -> c h x", h=2, x=3))
        load_x(0, 0, 2 * T)
        nc.sync.dma_start(offsets[:], offs)
        load_x(1, 0, T + MIDDLE_CUT)
        load_x(1, T + MIDDLE_CUT, 2 * T)
        load_w8_scales(0)
        load_x(2, 0, T + MIDDLE_CUT)
        load_w4_scales(0, 2, range(1))
        load_x(2, T + MIDDLE_CUT, 2 * T)
        load_x(3, T, 2 * T)
        load_x(3, LAST_CUT, T)
        load_x(3, 0, LAST_CUT)
        load_w4_scales(0, 2, range(1, 4))
        for g in range(2):
            load_w8(g)
            load_w4(g)
        load_w4_scales(2, E, range(4))
        load_w8(2)
        load_w8_scales(1)
        load_w4(2)

        windows = []
        for m in range(N_BLOCKS):
            windows.append(keep.tile([P, T], F32, name="window%d" % m, align_bytes=LONG_ROWS))
            if m < N_BLOCKS - 1:
                nc.vector.memset(windows[m][:], 0.0)
            else:
                nc.scalar.activation(windows[m][:], windows[0][:], COPY)

        make_identity(nc, identity[:])
        for h in range(2):
            spread = psum.tile([P, 3, P], F32, name="spread%d" % h, tag="bank%d" % (6 + h))
            for x in range(3):
                nc.tensor.transpose(spread[:, x, :], gate_columns[:, h, x : x + 1].to_broadcast([P, P]), identity[:])
            half = gates[:, h * S // 2 : (h + 1) * S // 2]
            copy = nc.vector.tensor_copy if h == 0 else nc.scalar.copy
            copy(out=half.rearrange("p (c x) -> p c x", x=3), in_=spread[:].rearrange("p x c -> p c x"))

        pairs = [keep.tile([P, T], U32, name="pair%d" % u, align_bytes=MX_ALIGN) for u in range(PAIRS)]
        picked = keep.tile([P, PAIRS, (E - 2) * C], U32, name="picked", align_bytes=MX_ALIGN)
        last_row = keep.tile([P, C], F32, name="last_row")

        pieces = [((0,), 0, 1), ((1,), 0, 1), ((0,), 2, 4), ((1,), 1, 2), ((1,), 2, 4), ((0,), 4, 6), ((1,), 4, 6), ((0,), 1, 2)]
        woven_at = {1: 8192, 2: 0, 4: 10240, 5: 0, 6: 0}
        codes_at = {7: 8192, 2: 8704, 4: 13312, 5: 10240, 6: 13824}
        second_gate = shared.tile([P, C], F32, name="second_gate", offset=13312, align_bytes=MX_ALIGN)
        woven, codes, planes, piece_of = [], [], [], {}
        for i, (passes, e0, e1) in enumerate(pieces):
            shape = [P, len(passes), (e1 - e0) * C]
            for a in passes:
                for e in range(e0, e1):
                    piece_of[a, e] = i
            if i in woven_at:
                woven.append(shared.tile(shape + [2], U32, name="woven%d" % i, offset=woven_at[i], align_bytes=MX_ALIGN)[:])
            else:
                woven.append(keep.tile(shape + [2], U32, name="woven%d" % i, align_bytes=MX_ALIGN)[:])
            if i in codes_at:
                codes.append(shared.tile(shape, U32, name="codes%d" % i, offset=codes_at[i], align_bytes=MX_ALIGN)[:])
            else:
                codes.append(keep.tile(shape, U32, name="codes%d" % i, align_bytes=MX_ALIGN)[:])
            planes.append(keep.tile(shape, U8, name="plane%d" % i, align_bytes=MX_ALIGN)[:])

        gate_copies = {
            (0, 1): woven[3][:, 0, :, 1].bitcast(F32),
            (0, 2): picked[:, 3, 3 * C // 2 : 5 * C // 2].bitcast(F32),
            (1, 1): second_gate[:],
        }

        for (e, m), copy_of_gate in gate_copies.items():
            nc.vector.tensor_copy(out=copy_of_gate, in_=gates[:, e * C : (e + 1) * C])

        def round_pair(pair, t0, t1, engine):
            halves = pairs[pair][:, t0:t1].bitcast(BF16).rearrange("p (t e) -> p t e", e=2)
            rows = raws[pair][:].rearrange("p (e t) -> p e t", e=2)[:, :, t0:t1]
            if engine == "gpsimd":
                nc.gpsimd.tensor_copy(out=halves, in_=rows.rearrange("p e t -> p t e"))
                return
            copy = nc.scalar.copy if engine == "scalar" else nc.vector.tensor_copy
            copy(out=halves.rearrange("p (c i) e -> p c e i", i=4), in_=rows.rearrange("p e (c i) -> p c e i", i=4))

        def gather(pair, e0, e1):
            nc.vector.tensor_copy(picked[:, pair, (e0 - 2) * C : (e1 - 2) * C], pairs[pair][:].indirect(listed(e0 * C, e1 * C)))

        def gather_woven(pair, i):
            passes, e0, e1 = pieces[i]
            nc.vector.tensor_copy(woven[i][:, 0, :, pair % 2], pairs[pair][:].indirect(listed(e0 * C, e1 * C)))

        def weave(i):
            passes, e0, e1 = pieces[i]
            rows = picked[:, 2 * passes[0] : 2 * passes[-1] + 2, (e0 - 2) * C : (e1 - 2) * C]
            nc.gpsimd.tensor_copy(out=woven[i], in_=rows.rearrange("p (a u) s -> p a s u", u=2))

        def quantise(i):
            values = woven[i].rearrange("p a s u -> p (a s u)").bitcast(BF16)
            nc.vector.quantize_mx(
                out=codes[i].rearrange("p a s -> p (a s)").bitcast(FP8X4),
                scales=planes[i].rearrange("p a s -> p (a s)"),
                in_=values,
            )

        def product(acc, e, m, a, start, stop):
            g = [h for h in range(len(WEIGHT_LOADS)) if WEIGHT_LOADS[h][0] <= e][-1]
            j = e - WEIGHT_LOADS[g][0]
            i = piece_of[a, e]
            passes, e0, e1 = pieces[i]
            cols = slice((e - e0) * C, (e - e0 + 1) * C)
            if a == 0:
                w_codes = w8[g][:, j, 4 * P * m : 4 * P * (m + 1)].bitcast(FP8X4)
                w_scale = w8_planes[e // 4][w8_row(e) :, P * m : P * (m + 1)]
            else:
                w_codes = w4[g][:, j, 2 * P * m : 2 * P * (m + 1)].bitcast(FP4X4)
                w_scale = w4_plane[:, e, P * m : P * (m + 1)]
            nc.tensor.matmul_mx(
                out=acc,
                lhsT=w_codes,
                lhsT_scale=w_scale,
                rhs=codes[i][:, passes.index(a), cols].bitcast(FP8X4),
                rhs_scale=planes[i][:, passes.index(a), cols],
                start=start,
                stop=stop,
            )

        results = keep.tile([P, N_BLOCKS * S], F32, name="results")
        units = [(1, e) for e in range(E)] + [(2, 0), (0, 0), (2, 1)] + [(0, e) for e in range(1, E)] + [(2, e) for e in range(2, E)]

        def result_columns(m, s0, count):
            at = units.index((m, s0 // C)) * C + s0 % C
            return results[:, at : at + count]

        def sums(e0, e1, blocks, bank):
            return psum.tile([P, len(blocks), (e1 - e0) * C], F32, name="acc%d_%d" % (e0, blocks[0]), tag="bank%d" % bank)

        def multiply(acc, e0, e1, blocks, a):
            parts = [(b, m, e) for b, m in enumerate(blocks) for e in range(e0, e1)]
            for b, m, e in parts:
                start = a == 0 and (b, m, e) == parts[0]
                stop = a == PASSES - 1 and (b, m, e) == parts[-1]
                product(acc[:, b, (e - e0) * C : (e - e0 + 1) * C], e, m, a, start, stop)

        def empty(acc, e0, e1, blocks):
            n = (e1 - e0) * C
            nc.vector.tensor_tensor(
                result_columns(blocks[0], e0 * C, len(blocks) * n).rearrange("p (b s) -> p b s", s=n),
                acc[:],
                gate_copies.get((e0, blocks[0]), gates[:, e0 * C : e1 * C]).unsqueeze(1).to_broadcast([P, len(blocks), n]),
                MULT,
            )

        def scatter(s0, s1, m, on_scalar):
            values = result_columns(m, s0, s1 - s0)
            if on_scalar:
                nc.scalar.activation(windows[m][:].indirect(listed(s0, s1)), values, COPY)
            else:
                nc.vector.tensor_copy(windows[m][:].indirect(listed(s0, s1)), values)

        round_pair(0, 0, FIRST_SHARE, "scalar")
        round_pair(0, FIRST_SHARE, T, "vector")
        gather(0, 2, E)
        gather_woven(0, 0)
        gather_woven(0, 7)
        for pair in (1, 2):
            early, late = MIDDLE_SHARES[pair]
            round_pair(pair, 0, early, "scalar")
            round_pair(pair, early, MIDDLE_CUT, "gpsimd")
            round_pair(pair, MIDDLE_CUT, late, "scalar")
            round_pair(pair, late, T, "gpsimd")
            if pair == 1:
                gather(1, 2, E)
                gather_woven(1, 0)
                gather_woven(1, 7)
                quantise(0)
        gather_woven(2, 1)
        gather_woven(2, 3)
        gather(2, 2, E)
        weave(2)

        first_values = woven[1][:, 0].rearrange("p s u -> p (s u)").bitcast(BF16)
        halves = (slice(0, C // 2), slice(C // 2, C))
        for half in halves:
            nc.scalar.activation(last_row[:, half], raws[3][:, T : 2 * T].indirect(listed(half.start, half.stop)), COPY)
        for half in halves:
            nc.scalar.copy(out=first_values[:, PACK * half.start + 3 : PACK * half.stop : PACK], in_=last_row[:, half])
        nc.scalar.activation(first_values[:, 2 : PACK * C : PACK], raws[3][:].indirect(listed(0, C)), COPY)
        round_pair(3, LAST_SHARE, T, "gpsimd")
        round_pair(3, 0, LAST_SHARE, "scalar")
        for i in (1, 7, 2):
            quantise(i)
        banks = {0: (([1], 0), ([2, 0], 1)), 1: (([1], 2), ([2, 0], 3)), 2: (([1], 4), ([2], 5), ([0], 6)), 3: (([1], 7), ([0], 0), ([2], 1))}
        accs = {}

        def first_passes(g):
            accs[g] = [sums(RUNS[g][0], RUNS[g][1], blocks, bank) for blocks, bank in banks[g]]
            for acc, (blocks, bank) in zip(accs[g], banks[g]):
                multiply(acc, RUNS[g][0], RUNS[g][1], blocks, 0)

        def finish(g, which):
            for i in which:
                multiply(accs[g][i], RUNS[g][0], RUNS[g][1], banks[g][i][0], 1)
                empty(accs[g][i], RUNS[g][0], RUNS[g][1], banks[g][i][0])

        for blocks, bank in banks[0]:
            acc = sums(0, 1, blocks, bank)
            for a in range(PASSES):
                multiply(acc, 0, 1, blocks, a)
            empty(acc, 0, 1, blocks)
        weave(5)
        first_passes(1)
        gather_woven(3, 3)
        quantise(3)
        gather(3, 2, 4)
        weave(4)
        gather(3, 4, 6)
        finish(1, range(2))
        first_passes(2)
        quantise(4)
        quantise(5)
        weave(6)
        for e, m in [(0, 1), (0, 0), (0, 2), (1, 1), (1, 2), (1, 0)]:
            scatter(e * C, (e + 1) * C, m, True)
        finish(2, range(3))
        quantise(6)
        scatter(2 * C, 4 * C, 1, True)
        scatter(2 * C, HANDED_BACK, 2, False)
        for blocks, bank in banks[3]:
            acc = sums(4, 6, blocks, bank)
            for a in range(PASSES):
                multiply(acc, 4, 6, blocks, a)
            empty(acc, 4, 6, blocks)
        scatter(4 * C, S, 1, True)
        scatter(2 * C, S, 0, False)
        scatter(HANDED_BACK, S, 2, True)
        for m in (1, 0, 2):
            nc.sync.dma_start(out=out[m * P : (m + 1) * P, :], in_=windows[m][:])
